import numpy as np, ml_dtypes
CORES = [9,25,41,57]
N = 4
BF = ml_dtypes.bfloat16
V, K, LA, LF, Q, RO, AS, FS = 4096, 1024, 256, 256, 4, 4, 170, 341
def lanes(flag, start, cap):
    order = (np.arange(K) + start) % K; fl = flag[:, order]
    o = np.argsort(~fl, axis=1, kind="stable")[:, :cap]
    return order[o], np.take_along_axis(fl, o, 1)
def judge(X, C, ids, T):
    n = ids.shape[1]; lit = np.take_along_axis(C, ids[:, None, :], 2); v = np.where(lit >= V, lit - V, lit)
    s = np.take_along_axis(X, v.reshape(8, 1, 16 * n), 2).reshape(8, 16, 16, n)
    s = np.where((lit >= V)[:, None], 63 - s, s)
    return lit, v, s, np.max(s, axis=2) < T
def states(rng, pa, pd):
    a = rng.choice(np.array(pa), (N, 8, 1)); b = rng.choice(np.array(pd), (N, 8, 1)); u = rng.random((N, 8, K))
    return np.where(u < a, 0, np.where(u >= 1 - b, 4, rng.integers(1, 4, (N, 8, K))))
def parts(rng):
    u = rng.random((N, 8, 16, K)); v = np.minimum((V * u * np.sqrt(u)).astype(np.int64), V - 1)
    T = rng.integers(58, 60, (N, 8, 1, 1)) + rng.integers(0, 2, (N, 8, 16, 1))
    return rng.integers(0, 64, (N, 8, 16, V)), v + V * rng.integers(0, 2, v.shape), states(rng, [0.3, 0.4, 0.5], [0.01, 0.05, 0.2]), T
def at(a, v):
    return np.take_along_axis(a, v.reshape(N, 8, -1), 2).reshape(v.shape)
def first(X, C, F, T):
    ia, ok = lanes(F == 0, 0, LA)
    return ia, ok & (np.sum(judge(X, C, ia, T)[3], axis=1) > Q)
def laid(rng, own, place, rest):
    X = np.zeros((8, 16, V), np.int64); C = np.zeros((8, 16, K), np.int64)
    for g in range(8):
        o = rng.permutation(V); sign = rng.integers(0, 2, V)
        s = rng.integers(0, rest[g] + 1, (16, V)); s[:, o[:K]] = own[g]
        X[g] = np.where(sign == 1, 63 - s, s)
        v = o[rng.integers(K, V, (16, K))]; v[place[g], np.arange(K)] = o[:K]
        C[g] = v + V * sign[v]
    return X, C
def full(rng):
    T = rng.integers(50, 61, (8, 16, 1)); own = rng.integers(10, 18, (8, 16, K)); place = rng.integers(0, 16, (8, K)); F = np.zeros((8, K), np.int64)
    own[[2, 7]] = 0; place[[2, 7]] = 0
    for g in range(8):
        o = rng.permutation(K); n = int(rng.integers(16, LF + 1))
        F[g, o[:n]] = rng.integers(1, 4, n); F[g, o[:16]] = 1
        own[g][:, o[:16]] = T[g] + rng.integers(0, 3, (16, 16))
    X, C = laid(rng, own, place, [9, 9, 0, 9, 9, 9, 9, 0])
    return X, C, F, T
def calm(rng):
    T = rng.integers(20, 51, (8, 16, 1)); own = np.repeat(T, K, axis=2); place = rng.integers(0, 16, (8, K)); F = rng.integers(1, 3, (8, K)); e = int(rng.integers(1, 4))
    for g in range(8):
        o = rng.permutation(K); n = 4 * int(rng.integers(2, LA >> 4)) + (e if g == 0 else 0); m = n + int(rng.integers(0, LA - n + 1)); h = m + ((K - m) >> 1)
        F[g, o[:m]] = 0
        own[g][:, o[n:h]] = 63; own[g][:, o[:n]] = T[g] - rng.integers(1, 6, (16, n))
    X, C = laid(rng, own, place, [9] * 8)
    return X, C, F, T
def pack(X, C, F, T):
    return {"xv": np.ascontiguousarray(X).reshape(N, 128, V).astype(np.float32).astype(BF), "cl": np.ascontiguousarray(C).reshape(N, 128, K).astype(np.int32),
            "fr": np.ascontiguousarray(F).astype(np.int32), "th": np.ascontiguousarray(T).reshape(N, 128, 1).astype(np.int32)}
def setup_inputs(rng):
    X, C, F, T = parts(rng)
    return pack(X, C, F, T)
def setup_inputs_spread(rng):
    low = np.minimum(np.exp2(6 * rng.random((N, 8, 1, V))) * rng.random((N, 8, 16, V)), 63).astype(np.int64)
    flip = rng.random((N, 8, V)) < 0.5; X = np.where(flip[:, :, None], 63 - low, low)
    u = rng.random((N, 8, 16, K)); v = np.minimum((V * u * u).astype(np.int64), V - 1)
    up = rng.random(v.shape) < rng.choice(np.array([0.0, 0.02, 0.06, 0.12]), (N, 8, 1, K))
    T = np.clip(61 - np.exp2(5.907 * rng.random((N, 8, 16, 1))).astype(np.int64), 1, 60)
    return pack(X, v + V * (at(flip, v) ^ up).astype(np.int64), states(rng, [0.1, 0.3, 0.6, 0.9], [0.0, 0.02, 0.3]), T)
def setup_inputs_ends(rng):
    X = 63 * rng.integers(0, 2, (N, 8, 16, V)); k = np.arange(16)[:, None]
    T = np.where(rng.random((N, 8, 16, 1)) < 0.75, 60, 1); T[:, [3, 7]] = 60; T[:, 0, 0] = 1
    u = rng.random((N, 8, K)); F = np.where(u < 0.45, 0, np.where(u < 0.75, 4, rng.choice(np.array([1, 3]), (N, 8, K))))
    m = rng.choice(np.array([16, 16, Q + 1, Q]), (N, 8, 1)); m[:, 1] = Q + 1; m[:, 2] = Q; m[:, [3, 7]] = 16
    low = np.argsort(np.argsort(rng.random((N, 8, 16)), axis=2), axis=2) < m
    X[..., 0] = np.where(low, 0, 63); X[..., V - 1] = np.where(low, 63, 0); X[..., 65] = 63
    sp = np.concatenate([np.arange(1, 65), np.arange(V - 65, V - 1)]); j = np.arange(128); cls = (j >> 1) % 3
    s = np.where(cls == 0, 59, np.where((cls == 2) & (k > Q), 63, 62)) - ((j // 6) % 2) * (k == j % 16)
    X[..., sp] = np.where(j % 2 == 1, 63 - s, s); lit = sp + V * (j % 2)
    C = np.where(rng.random((N, 8, 16, K)) < rng.choice(np.array([0.0, 0.5, 0.5, 1.0]), (N, 8, 1, K)), 0, 2 * V - 1)
    kind = rng.choice(np.array([0, 0, 0, 0, 0, 0, 0, 1, 2, 3]), (N, 8, K)); frm = rng.integers(0, 16, (N, 8, K))
    for q in range(N):
        F[q, 7] = 4; kind[q, 7] = rng.choice(np.array([0, 0, 1]), K)
        b = np.append(np.sort(AS + rng.permutation(K - 1 - AS)[:LA - 1]), K - 1)
        F[q, 7, rng.permutation(AS)[:32]] = 0; F[q, 7, b] = 0
        kind[q, 7, b[-32:]] = 2; kind[q, 7, b[-2:]] = 3; frm[q, 7, b[-2:]] = 0
    for c in range(3):
        a = lit[cls == c]; fill = a[rng.integers(0, len(a), C.shape)]
        C = np.where((kind == c + 1)[:, :, None] & (k >= frm[:, :, None]), fill, C)
    for q in range(N):
        ia, bad = first(X[q], C[q], F[q], T[q]); b = np.flatnonzero(bad[3])[:(int(np.sum(bad)) - 3) % 4]
        C[q, 3, 8, ia[3, b]] = 65
    return pack(X, C, F, T)
def setup_inputs_corners(rng):
    X, C, F, T = parts(rng); w = rng.random((N, 8, 1, K)); e = np.array([0, V - 1, V, 2 * V - 1])
    C = np.where(w < 0.15, rng.choice(e, (N, 8, 1, K)), np.where(w < 0.3, np.arange(K) + V * rng.integers(0, 2, (N, 8, 1, K)), np.where(w < 0.45, rng.choice(e, (N, 8, 16, K)), C)))
    T[:, 1] = np.where(rng.random((N, 16, 1)) < 0.3, 1, 60); T[:, 5] = 1; T[:, 6] = 60
    cases = ((0, K), (K, 0), (LA, LF), (LA + 1, LF + 1), (LA - 1, LF - 1), (1, 0), (2, K - 2), (0, 0))
    for q in range(N):
        for g in range(8):
            na, nz = cases[(g + q) % 8]; o = rng.permutation(K)
            F[q, g] = 4; F[q, g, o[:na]] = 0; F[q, g, o[na:na + nz]] = rng.integers(1, 4, nz)
    for q in range(0, N - 1, 2):
        bad = first(X[q], C[q], F[q], T[q])[1]; n = np.sum(bad[:, 0::2] & bad[:, 1::2], axis=1); c = 0
        for g in range(8):
            if n[g] < 2: continue
            d = int(n[g]) + (0, 1, -1)[c % 3]; c += 1
            z = rng.integers(0, 4, K); z[rng.permutation(K)[:d]] = 4; F[q + 1, g] = z
    return pack(X, C, F, T)
def setup_inputs_ties(rng):
    b = rng.choice(np.array([9, 30, 60]), (N, 8, 1, 1)); T = np.zeros((N, 8, 16, 1), np.int64) + b; i = np.arange(16)[:, None]
    mul = 2 * rng.integers(0, 8, (N, 8, 1, V)) + 1; sh = rng.integers(0, 16, (N, 8, 1, V)); n = Q + rng.integers(0, 2, (N, 8, 1, V))
    odd = np.arange(V) % 2 == 1
    s = np.where(odd & ((i * mul + sh) % 16 >= n), b + rng.integers(0, 4, (N, 8, 1, V)), b - 1 - rng.integers(0, 2, (N, 8, 1, V)))
    flip = rng.random((N, 8, V)) < 0.5; X = np.where(flip[:, :, None], 63 - s, s)
    lim = rng.choice(np.array([V // 2, V // 2, V // 16]), (N, 8, 1, 1))
    v = 2 * np.minimum((rng.random((N, 8, 16, K)) * lim).astype(np.int64), lim - 1)
    one = (i == rng.integers(0, 16, (N, 8, 1, K))) & (rng.random((N, 8, 1, K)) < 0.9)
    v = np.where(one, 2 * rng.integers(0, V // 2, v.shape) + 1, v)
    return pack(X, v + V * at(flip, v).astype(np.int64), states(rng, [0.3, 0.4, 0.5], [0.02, 0.1, 0.2]), T)
def setup_inputs_alike(rng):
    X, C, F, T = parts(rng); few = rng.integers(0, V, (N, 8, 24)); few[:, :, 0] = 0; few[:, :, 1] = V - 1
    v = np.take_along_axis(few, rng.integers(0, 24, (N, 8, 16 * K)), 2).reshape(N, 8, 16, K) + V * rng.integers(0, 2, (N, 8, 16, K))
    C[:, ::2] = v[:, ::2]
    for q in range(N): C[q, 5] = C[q, 5][:, rng.integers(0, 8, K)]
    o = rng.permutation(N)
    X[o[0]], C[o[0]], F[o[0]], T[o[0]] = full(rng)
    X[o[1]], C[o[1]], F[o[1]], T[o[1]] = calm(rng)
    return pack(X, C, F, T)
def check_inputs(d):
    bad = []
    for k, lo, hi in (("xv", 0, 63), ("cl", 0, 2 * V - 1), ("fr", 0, 4), ("th", 1, 60)):
        a = np.asarray(d[k]).astype(np.float64)
        if not np.all((a >= lo) & (a <= hi)): bad.append("range of " + k)
        elif not np.all(a == np.floor(a)): bad.append("whole numbers of " + k)
    return bad
def reference(xv, cl, fr, th):
    X = xv.astype(np.float32).astype(np.int64).reshape(N, 8, 16, V); C = cl.astype(np.int64).reshape(N, 8, 16, K); F = fr.astype(np.int64).reshape(N, 8, K)
    TH = th.astype(np.int64).reshape(N, 8, 16, 1); A = np.zeros(N, np.int64)
    for t in range(RO):
        nX = np.array(X); nC = np.array(C); nF = np.array(F); sent = []
        for r in range(N):
            T = TH[r] + (A[r] & 3)
            ia, oka = lanes(F[r] == 0, AS * t % K, LA); iz, okz = lanes((F[r] >= 1) & (F[r] <= 3), FS * t % K, LF)
            lit, v, s, fail = judge(X[r], C[r], ia, T); bad = oka & (np.sum(fail, axis=1) > Q); A[r] = np.sum(bad)
            m = oka & ~bad; nF[r][np.nonzero(m)[0], ia[m]] = 1
            wake = np.sum(judge(X[r], C[r], iz, T)[3], axis=1) > Q
            old = np.take_along_axis(F[r], iz, 1); nF[r][np.nonzero(okz)[0], iz[okz]] = np.where(wake, 0, old + 1)[okz]
            kk = np.argmax(np.sum(s * fail[:, :, None, :], axis=1), axis=1)[:, None, :]
            pick = np.take_along_axis(lit, kk, 1); pv = np.take_along_axis(v, kk, 1)[:, 0]
            up = np.minimum(np.take_along_axis(s, kk[:, None], 2)[:, :, 0] + 8, 63); new = np.where(pick >= V, 63 - up, up)
            for g in range(8):
                b = np.flatnonzero(bad[g]); u, ix = np.unique(pv[g, b], return_index=True); w = b[ix]
                nX[r, g][:, u] = np.where(fail[g][:, w], new[g][:, w], X[r, g][:, u])
            tot = np.sum(s, axis=1)
            sent.append((bad[:, 0::2] & bad[:, 1::2], np.where(tot[:, :, 1::2] > tot[:, :, 0::2], lit[:, :, 1::2], lit[:, :, 0::2])))
        for r in range(N):
            a = (r + 1 + t % 3) % N; both, joint = sent[r]
            for g in range(8):
                come = joint[g][:, both[g]]; dead = np.flatnonzero(F[a, g] == 4); n = min(come.shape[1], len(dead))
                nC[a, g][:, dead[:n]] = come[:, :n]; nF[a, g][dead[:n]] = 0
        X = nX; C = nC; F = nF
    return {"yx": X.reshape(N, 128, V).astype(np.float32).astype(BF), "yc": C.reshape(N, 128, K).astype(np.float32), "yf": F.astype(np.float32)}

@@ -1,0 +1,462 @@
+from concourse.mybir import AluOpType as OP, AxisListType, ActivationFunctionType as AF
+
+F4, B2, I4, U2 = "float32", "bfloat16", "int32", "uint16"
+SB = {
+    "xt": ([128, 8720], B2), "ci": ([128, 1024], I4), "cb": ([128, 1024], F4), "w": ([128, 3072], F4), "rw": ([128, 3072], B2),
+    "thi": ([128, 1], I4), "thf": ([128, 1], F4), "thr": ([128, 1], F4), "fr0": ([64, 128], I4), "frb": ([64, 128], B2),
+    "fn": ([128, 64], B2), "y": ([128, 64], B2), "fl": ([128, 198], B2), "sc": ([128, 198], F4), "zz": ([128, 198], F4),
+    "pf": ([128, 64], F4), "pos": ([128, 64], U2), "fo": ([64, 128], F4),
+    "lua": ([128, 256], U2), "luz": ([128, 256], U2), "sa": ([128, 4096], B2), "sz": ([128, 4096], B2), "mx": ([128, 4096], B2), "mz": ([128, 4096], B2),
+    "fa": ([128, 256], B2), "fz": ([128, 256], B2), "sm": ([128, 4096], B2), "vi": ([128, 256], B2),
+    "li": ([128, 256], I4), "hi": ([128, 256], I4), "lo": ([128, 256], I4), "ab": ([128, 512], F4), "at": ([128, 512], F4), "scn": ([128, 512], F4),
+    "di": ([128, 32], I4), "fti": ([128, 32, 8], I4), "ftb": ([128, 32, 8], B2), "fe": ([128, 16, 16], B2), "bd": ([128, 16, 128], B2),
+    "ddi": ([128, 48], I4), "db": ([128, 48], B2), "cu": ([128, 16], U2), "cc": ([128, 32], F4), "ge": ([128, 16], F4), "cm": ([128, 16], F4),
+    "tg": ([128, 16], F4), "tg0": ([128, 16], F4), "win": ([128, 16], F4), "wm": ([128, 32], F4), "of1": ([128, 32], F4), "of2": ([128, 32], F4), "off": ([128, 32], U2),
+    "sch": ([128, 256], B2), "nv": ([128, 512], B2), "junk": ([128, 2432], B2), "vs": ([128, 1], F4), "ai": ([128, 2], I4),
+    "dj": ([128, 128], F4), "jt": ([128, 128], F4), "ce": ([128, 128], B2), "o32": ([128, 128], B2),
+    "jo": ([128, 8], U2), "jw": ([128, 1024], F4), "jl": ([128, 512], F4), "rg": ([128, 1024], B2),
+    "im": ([128, 128], F4), "img": ([128, 128], F4), "g8": ([128, 8], F4), "ki": ([128, 8], I4), "kf": ([128, 8], F4), "kx": ([128, 32], F4),
+    "gi": ([128, 8], B2), "gif": ([128, 8], F4), "mb": ([128, 8], F4), "cbm": ([128, 8], F4), "bb": ([128, 128], B2), "bb9": ([128, 128], B2), "gt": ([128, 128], B2), "lt": ([128, 128], B2),
+    "id": ([128, 128], B2), "idm": ([128, 128], B2), "id8": ([128, 128], B2), "dg": ([128, 128], B2), "sel": ([128, 2048], B2), "nsel": ([128, 2048], B2), "qm": ([128, 1024], B2),
+    "lw0": ([128, 16], F4), "lw": ([128, 16], F4), "tg1": ([128, 16], F4), "bias": ([128, 16], F4), "tr": ([128, 32], F4), "l70": ([128, 16], F4),
+    "nc": ([128, 128], B2), "jc0": ([128, 8], F4), "jc1": ([128, 8], F4), "jc8": ([128, 8], B2), "mk": ([128, 4096], B2), "mk3": ([128, 198], B2), "one": ([128, 256], B2), "onf": ([128, 128], F4),
+}
+SCRATCH = {"q_" + k: ("sbuf", v[0], v[1]) for k, v in SB.items()}
+SCRATCH.update({"q_p%d" % i: ("psum", [128, 512], F4) for i in range(8)})
+NDMA = 40
+SEMAPHORES = ["ev", "es", "et", "eg"] + ["a%d" % t for t in range(4)] + ["l%d" % t for t in range(4)] + ["d%d" % i for i in range(NDMA)]
+XW0, XE = 512, 8720
+ZB, DB0, WW = 1024, 2048, 3072
+NS = 176
+TOT = 8
+BDS = (3, 4, 5, 6, 7)
+DED = (("s", 0, (15, 14)), ("v", 2, (9, 8, 7)), ("s", 7, (13, 12)), ("s", 3, (11, 10)), ("v", 4, (6, 5, 4, 3)), ("v", 5, (2, 1, 0)))
+SCOLS = tuple(a for e, b, aa in DED if e == "s" for a in aa)
+
+
+def rank_program(g, core, T, topo):
+    rank = T.rank_of(core)
+    if rank is None:
+        return
+    Q = {"v": g.vector, "s": g.scalar, "t": g.tensor, "g": g, "y": g.sync}
+    cnt = {q: 0 for q in Q}
+    know = {q: {} for q in Q}
+    snap, log, nd = {}, {}, [0]
+
+    def r(n, lo=None, hi=None, step=1, P=128):
+        t = T["q_" + n]
+        hi = t.shape[1] if hi is None else hi
+        lo = 0 if lo is None else lo
+        return (n, t[0:P, lo:hi:step] if step != 1 else t[0:P, lo:hi], lo, hi, step)
+
+    def r3(n, a, b=slice(None), lo=0, hi=1 << 20, st=1):
+        t = T["q_" + n]
+        return (n, t[:, a, b], lo, hi, st)
+
+    def ind(w, o):
+        return ("@", w, o)
+
+    def over(a, b):
+        if a[0] >= b[1] or b[0] >= a[1]:
+            return False
+        return not (a[2] == b[2] and a[2] > 1 and (a[0] - b[0]) % a[2])
+
+    def need(q, src, n):
+        k = know[q]
+        if k.get(src, 0) >= n:
+            return
+        Q[q].wait_ge(T.sem[src], n)
+        k[src] = n
+        for s2, n2 in snap.get((src, n), {}).items():
+            if k.get(s2, 0) < n2:
+                k[s2] = n2
+
+    def deps(q, acc):
+        req = {}
+        own = "e" + q
+        for (b, lo, hi, st, w) in acc:
+            bank = b[0] == "p" and len(b) == 2
+            for (src, l2, h2, s2, w2), n in log.get(b, {}).items():
+                if src == own:
+                    if not (w or w2) or (w and q == "t") or not over((lo, hi, st), (l2, h2, s2)):
+                        continue
+                elif not bank and (not (w or w2) or not over((lo, hi, st), (l2, h2, s2))):
+                    continue
+                if req.get(src, 0) < n:
+                    req[src] = n
+        for src in sorted(req, key=lambda x: (x[0] != "e", x)):
+            need(q, src, req[src])
+
+    def note(src, n, acc):
+        for (b, lo, hi, st, w) in acc:
+            log.setdefault(b, {})[(src, lo, hi, st, w)] = n
+
+    def flat(args, kw):
+        acc, real, kk = [], [], {}
+        for i, a in enumerate(args):
+            if isinstance(a, tuple) and a[0] == "@":
+                acc.append((a[1][0],) + a[1][2:] + (i == 0,))
+                acc.append((a[2][0],) + a[2][2:] + (False,))
+                real.append(a[1][1].indirect(a[2][1]))
+            elif isinstance(a, tuple):
+                acc.append((a[0],) + a[2:] + (i == 0,))
+                real.append(a[1])
+            else:
+                real.append(a)
+        for k, a in kw.items():
+            if isinstance(a, tuple):
+                acc.append((a[0],) + a[2:] + (k == "accum_out",))
+                kk[k] = a[1]
+            else:
+                kk[k] = a
+        return acc, real, kk
+
+    def do(q, name, *args, **kw):
+        acc, real, kk = flat(args, kw)
+        deps(q, acc)
+        e = Q[q]
+        f = {"copy": lambda: e.tensor_copy(*real), "tt": lambda: e.tensor_tensor(*real), "ts": lambda: e.tensor_scalar(*real),
+             "set": lambda: e.memset(*real), "red": lambda: e.tensor_reduce(*real), "scan": lambda: e.tensor_tensor_scan(*real),
+             "vt": lambda: e.transpose(*real), "act": lambda: e.activation(*real, **kk), "mm": lambda: e.matmul(*real),
+             "iota": lambda: e.iota(*real, **kk)}[name]
+        cnt[q] += 1
+        src = "e" + q
+        f().then_inc(T.sem[src], 1)
+        snap[(src, cnt[q])] = dict(know[q])
+        note(src, cnt[q], acc)
+
+    def dma(q, out, in_):
+        acc = []
+        for i, a in enumerate((out, in_)):
+            if isinstance(a, tuple):
+                acc.append((a[0],) + a[2:] + (i == 0,))
+        deps(q, acc)
+        x = "d%d" % nd[0]
+        nd[0] += 1
+        ap = [a[1] if isinstance(a, tuple) else a for a in (out, in_)]
+        Q[q].dma_start(ap[0], ap[1]).then_inc(T.sem[x], 16)
+        snap[(x, 16)] = dict(know[q])
+        note(x, 16, acc)
+
+    def v(*a): do("v", *a)
+    def pe(*a): do("t", "mm", *a)
+    def act(out, in_, f=AF.Copy, **k): do("s", "act", out, in_, f, **k)
+
+    def ts(out, in0, s1, op0, s2=None, op1=None):
+        if op1 is None:
+            v("ts", out, in0, s1, None, op0)
+        else:
+            v("ts", out, in0, s1, s2, op0, op1)
+
+    def iota(out, pat, base, ch):
+        if out[0] == "ki":
+            do("g", "iota", out, pat, base, ch)
+        else:
+            do("g", "iota", out, pat, base, ch, allow_small_or_imprecise_dtypes=True)
+
+    for gr in range(8):
+        dma("y" if gr % 2 == 0 else "s", r("fr0", 16 * gr, 16 * gr + 16, P=64), T.fr[gr:gr + 1, :])
+    dma("s", r("ci"), T.cl[:, :])
+    for i in range(2):
+        dma("y", r("xt", XW0 + 2048 * i, XW0 + 2048 * i + 2048), T.xv[:, 2048 * i:2048 * i + 2048])
+    dma("s", r("thi"), T.th[:, :])
+
+    iota(r("ki", 0, 1), [[1, 1]], 0, 1)
+    iota(r("im"), [[1, 128]], 0, 0)
+    iota(r("img"), [[1, 8], [0, 16]], 0, 0)
+    iota(r("g8"), [[1, 8]], 0, 0)
+    iota(r("lw0"), [[16, 16]], 0, 0)
+    iota(r("w"), [[0, WW]], 8192, 0)
+    iota(r("l70"), [[-32, 8], [0, 2]], 0, 0)
+    iota(r("jc0"), [[16, 8]], 0, 0)
+    iota(r("nc"), [[1, 128]], -255, 0)
+    iota(r("sel"), [[0, 2048]], 0, 0)
+    iota(r("jw"), [[0, 1024]], -20, 0)
+    iota(r("rw"), [[0, WW]], 1, 0)
+    kx = lambda i: r("kx", i, i + 1)
+    v("set", r("fl"), 0.0)
+    v("set", r("fl", 66, 67), 64.0)
+    v("set", r("fl", 132, 133), 128.0)
+    v("set", r("mk3"), 1.0)
+    v("set", r("mk3", 0, 198, 66), 0.0)
+    v("set", kx(7), -32.0)
+    v("set", kx(20), -36.0)
+    v("set", kx(21), 63.0)
+    v("set", r("mk"), 1.0)
+    v("set", r("mk", 0, 4096, 16), 0.0)
+    ts(r("ki", 1, 2), r("ki", 0, 1), 15, OP.bitwise_and)
+    ts(r("ki", 2, 3), r("ki", 0, 1), 4, OP.arith_shift_right)
+    ts(r("ki", 3, 4), r("ki", 0, 1), 31, OP.bitwise_and)
+    ts(r("ki", 4, 5), r("ki", 0, 1), 4, OP.arith_shift_right, 1, OP.bitwise_and)
+    v("copy", r("kf", 0, 5), r("ki", 0, 5))
+    pc, qc, gc, p31, hb = [r("kf", i, i + 1) for i in range(5)]
+    ts(r("id"), r("im"), pc, OP.is_equal)
+    ts(r("bb"), r("img"), gc, OP.is_equal)
+    ts(r("gt"), r("im"), pc, OP.is_gt)
+    v("tt", r("lt"), r("gt"), r("bb"), OP.mult)
+
+    def rank_stage(t, xw):
+        ts(r("fn"), xw, 16.0 if t else 0.0, OP.add, 0.0, OP.max)
+        act(r("y"), r("fn"), AF.Square, bias=kx(7))
+
+        def flags(seg, src, thr, st, ki):
+            c0 = st // 16
+            if st == 0:
+                ts(r("fl", seg + 1, seg + 65), r(src), thr, OP.is_lt)
+                return
+            if c0 < 63:
+                ts(r("fl", seg + 2, seg + 65 - c0), r(src, c0 + 1, 64), thr, OP.is_lt)
+            ts(r("fl", seg + 65 - c0, seg + 65), r(src, 0, c0), thr, OP.is_lt)
+            ts(r("fl", seg + 1, seg + 2), r(src, c0, c0 + 1), thr, OP.is_lt, kx(ki), OP.mult)
+            ts(r("fl", seg + 65, seg + 66), r(src, c0, c0 + 1), thr, OP.is_lt, kx(ki + 1), OP.mult)
+        a0, z0 = (170 * t) % 1024, (341 * t) % 1024
+        flags(0, "fn", 8.0, a0, 8 + (t - 1) * 4)
+        ts(r("fl", 133, 197), r("fn"), 56.0, OP.is_gt)
+        flags(66, "y", 512.0, z0, 10 + (t - 1) * 4)
+        pe(r("p5", 256, 454), r("bb"), r("fl"), True, True)
+        pe(r("p5", 0, 198), r("lt"), r("fl"), True, True)
+        v("scan", r("sc"), r("mk3"), r("p5", 256, 454), 0.0, OP.mult, OP.add)
+        v("tt", r("p6", 256, 453), r("sc", 0, 197), r("p5", 1, 198), OP.add)
+        v("tt", r("zz", 0, 197), r("p6", 256, 453), r("fl", 1, 198), OP.mult)
+
+        def add(lo, hi, src, at):
+            if hi > lo:
+                v("tt", r("pf", lo, hi), r(src[0], src[1] + lo, src[1] + hi), r("zz", at, at + hi - lo), OP.add)
+
+        def merge(seg, st, src):
+            c0 = st // 16
+            if st == 0:
+                add(0, 64, src, seg)
+                return
+            add(c0 + 1, 64, src, seg + 1)
+            add(0, c0, src, seg + 64 - c0)
+            add(c0, c0 + 1, src, seg)
+            add(c0, c0 + 1, ("pf", 0), seg + 64)
+        merge(0, a0, ("zz", 132))
+        merge(66, z0, ("pf", 0))
+        v("copy", r("pos"), r("pf"))
+
+    def consts_a():
+        ts(r("gi"), r("g8"), gc, OP.is_equal)
+        v("set", r("one"), 1.0)
+        v("set", r("onf"), 1.0 / 4096)
+        v("set", r("ce", 0, 1), 0.0)
+        v("set", r3("ftb", slice(1, 32, 2), 7, 15, 256, 16), 0.0)
+        ts(r("bb9"), r("img"), gc, OP.is_equal, -9.0, OP.mult)
+        ts(r("idm"), r("im"), pc, OP.is_equal, 8192.0, OP.mult)
+
+    def consts_b():
+        ts(kx(0), qc, -512.0, OP.mult, 7680.0, OP.add)
+        ts(kx(2), hb, -1.0, OP.mult, 1.0, OP.add)
+        ts(kx(3), qc, 7.0, OP.is_equal)
+        ts(kx(5), pc, 16.0, OP.add)
+        ts(kx(6), pc, -16.0, OP.add)
+        ts(kx(4), kx(3), -256.0, OP.mult, 256.0, OP.add)
+        ts(r("dg"), r("im"), pc, OP.is_equal, kx(0), OP.mult)
+        ts(r("id8"), r("im"), pc, OP.is_equal, 8.0, OP.mult)
+        for t in range(1, 4):
+            for c, st in enumerate(((170 * t) % 1024, (341 * t) % 1024)):
+                ts(kx(8 + (t - 1) * 4 + 2 * c), qc, float(st % 16), OP.is_ge)
+                ts(kx(9 + (t - 1) * 4 + 2 * c), qc, float(st % 16), OP.is_lt)
+        ts(r("gif"), r("g8"), gc, OP.is_equal)
+        ts(r("mb"), r("gif"), kx(4), OP.mult)
+        ts(r("cbm"), r("gif"), kx(3), OP.mult)
+        for a2 in range(2):
+            for g2 in range(2):
+                x = (pc, kx(5), kx(6))[(g2 - a2) % 3]
+                i = (a2 * 2 + g2) * 256
+                ts(r("qm", i, i + 128), r("im"), x, OP.is_equal, (kx(2), hb)[a2], OP.mult)
+                ts(r("qm", i + 128, i + 256), r("qm", i, i + 128), 64.0, OP.mult)
+        ts(r("lw"), r("lw0"), qc, OP.add)
+        ts(r("tg1"), r("lw"), -1.0, OP.mult, 3585.0, OP.add)
+        for a in SCOLS:
+            v("set", r("tg1", a, a + 1), 1.0)
+        ts(r("bias"), r("lw"), -3584.0, OP.add)
+        v("copy", r("tr", 0, 16), r("lw"))
+        ts(r("tr", 16, 32), r("lw"), 256.0, OP.add)
+        ts(r3("ftb", slice(0, 32, 2), 7, 7, 256, 16), r("l70"), p31, OP.subtract)
+        ts(r("jc1"), r("jc0"), qc, OP.add)
+        ts(r("jc8"), r("jc1"), -4096.0, OP.mult, 4096.0 * 255, OP.add)
+        v("copy", r("thf"), r("thi"))
+        v("copy", r("thr"), r("thi"))
+
+    ts(r("frb", P=64), r("fr0", P=64), 16.0, OP.mult)
+    pe(r("p6", 0, 64), r("frb", P=64), ("id", T.q_id[0:64, 0:64], 0, 64, 1), True, True)
+    v("set", r("xt", 8704, 8720), 63.0)
+    rank_stage(0, r("p6", 0, 64))
+    POS = r("pos")
+    XG = r("xt", XW0, XE)
+    for i in range(2):
+        act(r("xt", 4608 + 2048 * i, 6656 + 2048 * i), r("xt", 512 + 2048 * i, 2560 + 2048 * i), AF.Identity, scale=-1.0, bias=kx(21))
+    consts_a()
+    consts_b()
+    v("copy", ind(r("w"), POS), r("ci"))
+    for q in range(16):
+        act(r("sel", q * 129, q * 128 + 128, 16), r("gi"))
+    act(r("nsel"), r("sel"), AF.Copy, scale=-1.0)
+
+    for t in range(4):
+        last = t == 3
+        dst = T.cores[(rank + 1 + t % 3) % len(T.cores)]
+        if t:
+            v("copy", ind(r("w"), POS), r("cb"))
+        v("copy", r("lua"), r("w", 0, 256))
+        act(r("sa", 0, 16 * NS), ind(XG, r("lua", 0, NS)))
+        v("copy", r("luz"), r("w", ZB, ZB + 256))
+        for i in range(2):
+            act(r("sz", 2048 * i, 2048 * i + 2048), ind(XG, r("luz", 128 * i, 128 * i + 128)))
+        if NS < 256:
+            v("copy", r("sa", 16 * NS, 4096), ind(XG, r("lua", NS, 256)))
+            v("scan", r("mx", 16 * NS, 4096), r("mk", 16 * NS, 4096), r("sa", 16 * NS, 4096), 0.0, OP.mult, OP.max)
+        v("copy", r("li"), r("w", 0, 256))
+        ts(r("hi"), r("li"), 6, OP.arith_shift_right)
+        ts(r("lo"), r("li"), 63, OP.bitwise_and)
+        v("tt", r("dj"), r("w", 1, 256, 2), r("w", 0, 256, 2), OP.subtract)
+        v("scan", r("mx", 0, 16 * NS), r("mk", 0, 16 * NS), r("sa", 0, 16 * NS), 0.0, OP.mult, OP.max)
+        ts(r("fa"), r("mx", 15, 4096, 16), r("thr"), OP.is_lt)
+
+        def totals(k0, k1):
+            for k in range(k0, k1):
+                pe(r("p3", 0, 128), r("sel", 128 * k, 128 * k + 128), r("sa", 16 + k, 4096, 32), k == 0, False)
+                pe(r("p3", 0, 128), r("nsel", 128 * k, 128 * k + 128), r("sa", k, 4096, 32), False, k == 15)
+
+        def product(k0, k1):
+            for k in range(k0, k1):
+                v("tt", r("sm", 256 * k, 256 * k + 256), r("sa", k, 4096, 16), r("p2", 0, 256), OP.mult)
+                pe(r("p0", 0, 256), r("sel", 128 * k, 128 * k + 128), r("sm", 256 * k, 256 * k + 256), False, k == 15)
+        totals(0, TOT)
+        pe(r("p0", 0, 256), r("dg"), r("one"), True, False)
+        pe(r("p2", 0, 256), r("idm"), r("fa"), True, True)
+        pe(r("p1", 0, 256), r("bb9"), r("fa"), True, True)
+        product(0, 4)
+        ts(r("vi"), r("p1", 0, 256), -40.0, OP.is_lt, 256.0, OP.mult)
+        act(r("rw", 0, 256), r("p1", 0, 256), AF.Relu, bias=kx(20), scale=-1.0)
+        pe(r("p0", 0, 256), r("id"), r("vi"), False, False)
+        product(4, 16)
+        totals(TOT, 16)
+        v("tt", r("ab", 0, 256), r("p0", 0, 256), r("hi"), OP.add)
+        v("tt", r("ab", 256, 512), r("p0", 0, 256), r("lo"), OP.add)
+        v("vt", r("at"), r("ab"))
+        v("scan", r("scn"), r("mk", 0, 512), r("at"), 0.0, OP.mult, OP.max)
+        for d in range(2):
+            v("copy", r("di", d, 32, 2), r("scn", 256 * d + 15, 256 * d + 256, 16))
+        for f in range(7):
+            ts(r3("fti", slice(None), f, f, 256, 8), r("di"), f if f < 6 else 8, OP.arith_shift_right, 1, OP.bitwise_and)
+        ts(r("ddi", 0, 16), r("di", 0, 32, 2), 127, OP.bitwise_and)
+        ts(r("ddi", 16, 32), r("di", 1, 32, 2), 63, OP.bitwise_and)
+        ts(r("ddi", 32, 48), r("di", 1, 32, 2), 8, OP.arith_shift_right, 1, OP.bitwise_and)
+        ts(r3("ftb", slice(None), slice(0, 7)), r3("fti", slice(None), slice(0, 7)), 2.0, OP.mult, -1.0, OP.add)
+        v("copy", r("db"), r("ddi"))
+        v("vt", r3("fe", slice(None)), r3("ftb", slice(None)))
+        for gr in range(8):
+            o = r3("bd", slice(None), slice(16 * gr, 16 * gr + 16), 16 * gr, 16 * gr + 16)
+            if gr in BDS:
+                act(o, r3("fe", slice(None)), AF.Identity, bias=r("cbm", gr, gr + 1), scale=r("mb", gr, gr + 1))
+            else:
+                ts(o, r3("fe", slice(None)), r("mb", gr, gr + 1), OP.mult, r("cbm", gr, gr + 1), OP.add)
+
+        def qmat(a2, g2, m):
+            i = (a2 * 2 + g2) * 256 + 128 * m
+            return r("qm", i, i + 128)
+        for a2 in range(2):
+            pe(r("p4", a2, 16, 2), qmat(a2, 0, 1), r("db", 0, 16, 2), True, False)
+            pe(r("p4", a2, 16, 2), qmat(a2, 1, 1), r("db", 1, 16, 2), False, False)
+            pe(r("p4", a2, 16, 2), qmat(a2, 0, 0), r("db", 16, 32, 2), False, False)
+            pe(r("p4", a2, 16, 2), qmat(a2, 1, 0), r("db", 17, 32, 2), False, True)
+            pe(r("p4", 16 + a2, 32, 2), qmat(a2, 0, 0), r("db", 32, 48, 2), True, False)
+            pe(r("p4", 16 + a2, 32, 2), qmat(a2, 1, 0), r("db", 33, 48, 2), False, True)
+        ts(r("p3", 128, 256), r("p3", 0, 128), 0.0, OP.is_gt)
+        v("tt", r("p3", 256, 384), r("dj"), r("p3", 128, 256), OP.mult)
+        v("tt", r("jt"), r("p3", 256, 384), r("w", 0, 256, 2), OP.add)
+        v("copy", r("cu"), r("p4", 0, 16))
+        act(r("sch"), ind(XG, r("cu")))
+        at = {}
+        for e, b, aa in DED:
+            o = 32 if b == 4 else 0
+            for a in aa:
+                at[a] = r("p%d" % b, o, o + 16 * (a + 1))
+                o += 16 * (a + 1)
+        for e, b, aa in DED[:4]:
+            for a in aa:
+                pe(at[a], r3("bd", a), r3("fe", slice(0, a + 1)), True, True)
+        v("tt", r("p5", 0, 128), r("vi", 0, 256, 2), r("vi", 1, 256, 2), OP.min)
+        v("scan", r("ce", 1, 128), r("one", 0, 127), r("p5", 0, 127), 0.0, OP.mult, OP.add)
+        v("tt", r("p5", 128, 256), r("p5", 0, 128), r("nc"), OP.mult)
+        v("tt", r("o32"), r("p5", 128, 256), r("ce"), OP.add)
+        pe(r("p6", 0, 8), r("id"), r("jc8"), True, False)
+        for q in range(16):
+            pe(r("p6", 0, 8), r("sel", 128 * q, 128 * q + 128), r("o32", q, 128, 16), False, q == 15)
+        ts(r("cc", 0, 16), r("p4", 0, 16), 512.0, OP.add)
+        ts(r("ge"), r("p4", 0, 16), 4096.0, OP.is_lt, 8192.0, OP.mult)
+        ts(r("cm"), r("p4", 0, 16), -3584.0, OP.add)
+        v("tt", r("tg0"), r("tg1"), r("p4", 16, 32), OP.mult)
+        v("tt", r("cc", 16, 32), r("ge"), r("cm"), OP.add)
+        ts(r("tg"), r("tg0"), -1.0, OP.add)
+        ts(r("jo"), r("p6", 0, 8), 1.0 / 4096, OP.mult)
+        v("copy", ind(r("jw", 256 * t, 256 * t + 256), r("jo")), r("jt"))
+        rid, pid, _ = topo.addr(dst)
+        deps("g", [("jw", 256 * t, 256 * t + 128, 1, False)])
+        g.remote_dma(T.q_jl[:, 128 * t:128 * t + 128], T.q_jw[:, 256 * t:256 * t + 128], T.sem["a%d" % t], T.sem["l%d" % t], pid, rid, topo.mask(core, dst))
+        src = T.cores[(rank - 1 - t % 3) % len(T.cores)]
+        note("a%d" % t, len(topo.engines(src, core)), [("jl", 128 * t, 128 * t + 128, 1, True)])
+        for e, b, aa in DED[4:]:
+            for a in aa:
+                pe(at[a], r3("bd", a), r3("fe", slice(0, a + 1)), True, True)
+        pe(r("p6", 256, 512), r("id8"), r("fa"), True, False)
+        pe(r("p6", 256, 512), r("id"), r("sch"), False, True)
+        for i in range(2):
+            v("scan", r("mz", 2048 * i, 2048 * i + 2048), r("mk", 0, 2048), r("sz", 2048 * i, 2048 * i + 2048), 0.0, OP.mult, OP.max)
+        ts(r("fz"), r("mz", 15, 4096, 16), r("thr"), OP.is_lt)
+        pe(r("p1", 256, 512), r("bb9"), r("fz"), True, True)
+        for e, b, aa in DED:
+            for a in aa:
+                if e == "v":
+                    v("red", r("win", a, a + 1), at[a], AxisListType.X, OP.max)
+                else:
+                    act(r("junk", 8 * a * (a + 1), 8 * (a + 1) * (a + 2)), at[a], AF.Relu, bias=r("bias", a, a + 1), accum_out=r("win", a, a + 1))
+        act(r("rw", ZB, ZB + 256), r("p1", 256, 512), AF.Relu, bias=kx(20), scale=-1.0)
+        act(r("nv", 256, 512), r("p6", 256, 512), AF.Relu, bias=kx(21), scale=-1.0)
+        ts(r("nv", 0, 256), r("p6", 256, 512), 63.0, OP.min)
+        jl = r("jl", 128 * t, 128 * t + 128)
+        ts(r("rw", DB0, DB0 + 128), jl, 9.0, OP.add, 1.0, OP.max)
+        ts(r("p5", 0, 128), jl, -0.5, OP.is_gt, -16384.0, OP.mult)
+        v("tt", r("p5", 128, 256), r("w", DB0, DB0 + 128), r("p5", 0, 128), OP.add)
+        v("tt", r("w", DB0, DB0 + 128), r("p5", 128, 256), jl, OP.max)
+        act(r("rg"), ind(r("rw"), POS))
+        if not last:
+            act(r("junk", 2176, 2432), r("vi"), AF.Copy, accum_out=r("vs"))
+        act(r("cb"), ind(r("w"), POS))
+        v("tt", r("wm", 0, 16), r("win"), r("tg"), OP.is_equal)
+        v("tt", r("wm", 16, 32), r("win"), r("tg"), OP.is_equal)
+        v("tt", r("of1"), r("cc"), r("wm"), OP.mult)
+        v("tt", r("of2"), r("of1"), r("tr"), OP.max)
+        v("copy", r("off"), r("of2"))
+        v("copy", ind(r("xt"), r("off")), r("nv"))
+        if last:
+            dma("y", T.yx[:, 0:2048], r("xt", XW0, XW0 + 2048))
+            dma("y", T.yx[:, 2048:4096], r("xt", XW0 + 2048, XW0 + 4096))
+        else:
+            for b in (0, ZB):
+                iota(r("w", b, b + 256), [[0, 256]], 8192, 0)
+        pe(r("p6", 0, 64), r("id"), r("fn"), True, False)
+        for q in range(16):
+            pe(r("p6", 0, 64), r("nsel", 128 * q, 128 * q + 128), r("rg", q, 1024, 16), False, q == 15)
+        if not last:
+            pe(r("p4", 300, 301), r("onf"), r("vs"), True, True)
+            rank_stage(t + 1, r("p6", 0, 64))
+            v("copy", r("ai", 0, 1), r("p4", 300, 301))
+            ts(r("ai", 1, 2), r("ai", 0, 1), 3, OP.bitwise_and)
+            v("tt", r("thr"), r("ai", 1, 2), r("thf"), OP.add)
+    dma("s", T.yc[:, :], r("cb"))
+    ts(r("fn"), r("p6", 0, 64), 16.0, OP.add, 0.0, OP.max)
+    pe(r("p5", 0, 128, P=64), r("fn"), r("id"), True, True)
+    ts(r("fo", P=64), r("p5", 0, 128, P=64), 1.0 / 16, OP.mult)
+    for gr in range(8):
+        dma("y" if gr % 2 == 0 else "s", T.yf[gr:gr + 1, :], r("fo", 16 * gr, 16 * gr + 16, P=64))
+    for q in "vstg":
+        need("g", "e" + q, cnt[q])
+    for i in range(nd[0]):
+        need("g", "d%d" % i, 16)
+    for t in range(4):
+        d = T.cores[(rank + 1 + t % 3) % len(T.cores)]
+        need("g", "l%d" % t, len(topo.engines(core, d)))

@@ -12,7 +12,7 @@ SB = {
     "di": ([128, 32], I4), "fti": ([128, 32, 8], I4), "ftb": ([128, 32, 8], B2), "fe": ([128, 16, 16], B2), "bd": ([128, 16, 128], B2),
     "ddi": ([128, 48], I4), "db": ([128, 48], B2), "cu": ([128, 16], U2), "cc": ([128, 32], F4), "ge": ([128, 16], F4), "cm": ([128, 16], F4),
     "tg": ([128, 16], F4), "tg0": ([128, 16], F4), "win": ([128, 16], F4), "wm": ([128, 32], F4), "of1": ([128, 32], F4), "of2": ([128, 32], F4), "off": ([128, 32], U2),
-    "sch": ([128, 256], B2), "nv": ([128, 512], B2), "junk": ([128, 2432], B2), "vs": ([128, 1], F4), "ai": ([128, 2], I4),
+    "sch": ([128, 256], B2), "nv": ([128, 512], B2), "junk": ([128, 2560], B2), "dra": ([128, 64], F4), "drb": ([128, 64], F4), "dr": ([128, 64], F4), "nt": ([128, 64], F4), "ns": ([128, 1], F4), "vs": ([128, 1], F4), "ai": ([128, 2], I4),
     "dj": ([128, 128], F4), "jt": ([128, 128], F4), "ce": ([128, 128], B2), "o32": ([128, 128], B2),
     "jo": ([128, 8], U2), "jw": ([128, 1024], F4), "jl": ([128, 512], F4), "rg": ([128, 1024], B2),
     "im": ([128, 128], F4), "img": ([128, 128], F4), "g8": ([128, 8], F4), "ki": ([128, 8], I4), "kf": ([128, 8], F4), "kx": ([128, 32], F4),
@@ -27,11 +27,13 @@ NDMA = 40
 SEMAPHORES = ["ev", "es", "et", "eg"] + ["a%d" % t for t in range(4)] + ["l%d" % t for t in range(4)] + ["d%d" % i for i in range(NDMA)]
 XW0, XE = 512, 8720
 ZB, DB0, WW = 1024, 2048, 3072
-NS = 176
-TOT = 8
-BDS = (3, 4, 5, 6, 7)
-DED = (("s", 0, (15, 14)), ("v", 2, (9, 8, 7)), ("s", 7, (13, 12)), ("s", 3, (11, 10)), ("v", 4, (6, 5, 4, 3)), ("v", 5, (2, 1, 0)))
+LS, LB = 96, 128
+BDS = (2, 3, 4, 5, 6, 7)
+DED = (("s", 0, (15, 14)), ("s", 7, (13, 12)), ("s", 3, (11, 10)), ("s", 2, (9, 8, 7)), ("v", 4, (6, 5, 4, 3, 2, 1, 0)))
 SCOLS = tuple(a for e, b, aa in DED if e == "s" for a in aa)
+
+
+CY, CPE, WAKE, FIX, SLACK, GAMMA, SIGMA = 0.00105, 0.0009, 0.12, 0.01, 0.05, 1.7, 3.5
 
 
 def rank_program(g, core, T, topo):
@@ -111,32 +113,119 @@ def rank_program(g, core, T, topo):
                 kk[k] = a
         return acc, real, kk
 
+    ops = []
+
+    def cols(a):
+        if a[0] == "@":
+            return 16 * cols(a[2])
+        return min(-(-(a[3] - a[2]) // a[4]), 256 if a[3] >= 1 << 20 else 1 << 20)
+
+    def cost(q, name, args):
+        xs = [a for a in args if isinstance(a, tuple)]
+        n = max(cols(a) for a in xs[1:]) if len(xs) > 1 else cols(xs[0])
+        names = [a[1][0] if a[0] == "@" else a[0] for a in xs]
+        two = all(b in SB and SB[b][1] in (B2, U2) for b in names)
+        if name == "mm":
+            return max(64, cols(args[2])) * (4 if SB[args[2][0]][1] == F4 else 1) * CPE
+        if name == "iota":
+            return 0.13 + 2 * cols(args[0]) * CY
+        if args[0][0] == "@":
+            n *= SIGMA
+        elif any(a[0] == "@" for a in xs):
+            n *= GAMMA
+        elif name == "tt":
+            n *= 1 if any(len(b) == 2 and b[0] == "p" for b in names) else 2
+        elif name in ("copy", "ts", "scan", "vt", "set") and two:
+            n *= 0.5
+        return max(n, 64) * CY + FIX
+
     def do(q, name, *args, **kw):
         acc, real, kk = flat(args, kw)
-        deps(q, acc)
         e = Q[q]
         f = {"copy": lambda: e.tensor_copy(*real), "tt": lambda: e.tensor_tensor(*real), "ts": lambda: e.tensor_scalar(*real),
              "set": lambda: e.memset(*real), "red": lambda: e.tensor_reduce(*real), "scan": lambda: e.tensor_tensor_scan(*real),
              "vt": lambda: e.transpose(*real), "act": lambda: e.activation(*real, **kk), "mm": lambda: e.matmul(*real),
              "iota": lambda: e.iota(*real, **kk)}[name]
-        cnt[q] += 1
-        src = "e" + q
-        f().then_inc(T.sem[src], 1)
-        snap[(src, cnt[q])] = dict(know[q])
-        note(src, cnt[q], acc)
+
+        def issue():
+            deps(q, acc)
+            cnt[q] += 1
+            src = "e" + q
+            f().then_inc(T.sem[src], 1)
+            snap[(src, cnt[q])] = dict(know[q])
+            note(src, cnt[q], acc)
+        c = cost(q, name, args)
+        ops.append((q, acc, c, c, issue))
 
     def dma(q, out, in_):
-        acc = []
+        acc, ap = [], []
         for i, a in enumerate((out, in_)):
+            ap.append(a[1] if isinstance(a, tuple) else a)
             if isinstance(a, tuple):
                 acc.append((a[0],) + a[2:] + (i == 0,))
-        deps(q, acc)
-        x = "d%d" % nd[0]
-        nd[0] += 1
-        ap = [a[1] if isinstance(a, tuple) else a for a in (out, in_)]
-        Q[q].dma_start(ap[0], ap[1]).then_inc(T.sem[x], 16)
-        snap[(x, 16)] = dict(know[q])
-        note(x, 16, acc)
+
+        def issue():
+            deps(q, acc)
+            x = "d%d" % nd[0]
+            nd[0] += 1
+            Q[q].dma_start(ap[0], ap[1]).then_inc(T.sem[x], 16)
+            snap[(x, 16)] = dict(know[q])
+            note(x, 16, acc)
+        ops.append((q, acc, 0.08, 2.5 + (acc[0][2] - acc[0][1]) / 1000, issue))
+
+    def order():
+        n = len(ops)
+        pre = [{} for _ in range(n)]
+        hist = {}
+        for i in range(n):
+            q, acc = ops[i][0], ops[i][1]
+            for (b, lo, hi, st, w) in acc:
+                bank = b[0] == "p" and len(b) == 2
+                hs = hist.setdefault(b, ([], []))
+                for h in (hs[0], hs[1]) if (w or bank) else (hs[0],):
+                    for (j, q2, l2, h2, s2, w2) in h:
+                        if bank and q == "t" and q2 == "t":
+                            pre[i].setdefault(j, 0.0)
+                        elif (bank and q != q2) or ((w or w2) and over((lo, hi, st), (l2, h2, s2))):
+                            pre[i][j] = WAKE
+            for (b, lo, hi, st, w) in acc:
+                hist[b][0 if w else 1].append((i, q, lo, hi, st, w))
+        post = [[] for _ in range(n)]
+        for i in range(n):
+            pre[i].pop(i, None)
+            for j in pre[i]:
+                post[j].append(i)
+        way = [0.0] * n
+        for i in range(n - 1, -1, -1):
+            way[i] = ops[i][3] + max([way[j] + pre[j][i] for j in post[i]], default=0.0)
+        left = [len(p) for p in pre]
+        ready = {q: {} for q in Q}
+        free = {q: 0.0 for q in Q}
+        end = [0.0] * n
+        for i in range(n):
+            if not left[i]:
+                ready[ops[i][0]][i] = 0.0
+        done = []
+        while len(done) < n:
+            best = None
+            for q in Q:
+                if ready[q]:
+                    t0 = min(max(free[q], x) for x in ready[q].values())
+                    i = max((i for i, x in ready[q].items() if max(free[q], x) <= t0 + SLACK), key=lambda k: way[k])
+                    s0 = max(free[q], ready[q][i])
+                    if best is None or s0 < best[0]:
+                        best = (s0, q, i)
+            s0, q, i = best
+            del ready[q][i]
+            free[q] = s0 + ops[i][2]
+            end[i] = s0 + ops[i][3]
+            done.append(i)
+            for j in post[i]:
+                left[j] -= 1
+                if not left[j]:
+                    ready[ops[j][0]][j] = max(end[k] + w for k, w in pre[j].items())
+        for i in done:
+            ops[i][4]()
 
     def v(*a): do("v", *a)
     def pe(*a): do("t", "mm", *a)
@@ -170,9 +259,8 @@ def rank_program(g, core, T, topo):
     iota(r("l70"), [[-32, 8], [0, 2]], 0, 0)
     iota(r("jc0"), [[16, 8]], 0, 0)
     iota(r("nc"), [[1, 128]], -255, 0)
-    iota(r("sel"), [[0, 2048]], 0, 0)
-    iota(r("jw"), [[0, 1024]], -20, 0)
     iota(r("rw"), [[0, WW]], 1, 0)
+    iota(r("jw"), [[0, 1024]], -20, 0)
     kx = lambda i: r("kx", i, i + 1)
     v("set", r("fl"), 0.0)
     v("set", r("fl", 66, 67), 64.0)
@@ -182,6 +270,7 @@ def rank_program(g, core, T, topo):
     v("set", kx(7), -32.0)
     v("set", kx(20), -36.0)
     v("set", kx(21), 63.0)
+    v("set", kx(22), 0.5)
     v("set", r("mk"), 1.0)
     v("set", r("mk", 0, 4096, 16), 0.0)
     ts(r("ki", 1, 2), r("ki", 0, 1), 15, OP.bitwise_and)
@@ -195,9 +284,17 @@ def rank_program(g, core, T, topo):
     ts(r("gt"), r("im"), pc, OP.is_gt)
     v("tt", r("lt"), r("gt"), r("bb"), OP.mult)
 
-    def rank_stage(t, xw):
-        ts(r("fn"), xw, 16.0 if t else 0.0, OP.add, 0.0, OP.max)
+    def new_states(t, xw):
+        if t == 0:
+            ts(r("fn"), xw, 0.0, OP.max)
+        else:
+            ts(r("p6", 64, 128), xw, 16.0, OP.add, 0.0, OP.max)
+            v("tt", r("fn"), r("p6", 64, 128), r("nt"), OP.mult)
+
+    def rank_stage(t, xw, then=lambda: None):
+        new_states(t, xw)
         act(r("y"), r("fn"), AF.Square, bias=kx(7))
+        then()
 
         def flags(seg, src, thr, st, ki):
             c0 = st // 16
@@ -237,7 +334,6 @@ def rank_program(g, core, T, topo):
         v("copy", r("pos"), r("pf"))
 
     def consts_a():
-        ts(r("gi"), r("g8"), gc, OP.is_equal)
         v("set", r("one"), 1.0)
         v("set", r("onf"), 1.0 / 4096)
         v("set", r("ce", 0, 1), 0.0)
@@ -246,6 +342,7 @@ def rank_program(g, core, T, topo):
         ts(r("idm"), r("im"), pc, OP.is_equal, 8192.0, OP.mult)
 
     def consts_b():
+        ts(r("nsel"), r("sel"), -1.0, OP.mult)
         ts(kx(0), qc, -512.0, OP.mult, 7680.0, OP.add)
         ts(kx(2), hb, -1.0, OP.mult, 1.0, OP.add)
         ts(kx(3), qc, 7.0, OP.is_equal)
@@ -280,6 +377,10 @@ def rank_program(g, core, T, topo):
         v("copy", r("thf"), r("thi"))
         v("copy", r("thr"), r("thi"))
 
+    ts(r("gi"), r("g8"), gc, OP.is_equal)
+    v("set", r("sel"), 0.0)
+    for q in range(16):
+        act(r("sel", q * 129, q * 128 + 128, 16), r("gi"))
     ts(r("frb", P=64), r("fr0", P=64), 16.0, OP.mult)
     pe(r("p6", 0, 64), r("frb", P=64), ("id", T.q_id[0:64, 0:64], 0, 64, 1), True, True)
     v("set", r("xt", 8704, 8720), 63.0)
@@ -289,51 +390,57 @@ def rank_program(g, core, T, topo):
     for i in range(2):
         act(r("xt", 4608 + 2048 * i, 6656 + 2048 * i), r("xt", 512 + 2048 * i, 2560 + 2048 * i), AF.Identity, scale=-1.0, bias=kx(21))
     consts_a()
-    consts_b()
     v("copy", ind(r("w"), POS), r("ci"))
-    for q in range(16):
-        act(r("sel", q * 129, q * 128 + 128, 16), r("gi"))
-    act(r("nsel"), r("sel"), AF.Copy, scale=-1.0)
 
     for t in range(4):
         last = t == 3
         dst = T.cores[(rank + 1 + t % 3) % len(T.cores)]
         if t:
             v("copy", ind(r("w"), POS), r("cb"))
-        v("copy", r("lua"), r("w", 0, 256))
-        act(r("sa", 0, 16 * NS), ind(XG, r("lua", 0, NS)))
+        for lo, hi in ((0, LS), (LS, 256)):
+            v("copy", r("lua", lo, hi), r("w", lo, hi))
+            if lo:
+                lo = LB
+            act(r("sa", 16 * lo, 16 * hi), ind(XG, r("lua", lo, hi)))
+        v("copy", r("sa", 16 * LS, 16 * LB), ind(XG, r("lua", LS, LB)))
         v("copy", r("luz"), r("w", ZB, ZB + 256))
         for i in range(2):
             act(r("sz", 2048 * i, 2048 * i + 2048), ind(XG, r("luz", 128 * i, 128 * i + 128)))
-        if NS < 256:
-            v("copy", r("sa", 16 * NS, 4096), ind(XG, r("lua", NS, 256)))
-            v("scan", r("mx", 16 * NS, 4096), r("mk", 16 * NS, 4096), r("sa", 16 * NS, 4096), 0.0, OP.mult, OP.max)
+        ts(r("dra"), r("zz", 132, 196), 1.0, OP.is_lt, 1e5, OP.mult)
+        ts(r("drb"), r("zz", 132, 196), 2.0, OP.mult, -4224.0, OP.add)
+        v("tt", r("dr"), r("dra"), r("drb"), OP.add)
+        if t == 0:
+            consts_b()
         v("copy", r("li"), r("w", 0, 256))
-        ts(r("hi"), r("li"), 6, OP.arith_shift_right)
         ts(r("lo"), r("li"), 63, OP.bitwise_and)
-        v("tt", r("dj"), r("w", 1, 256, 2), r("w", 0, 256, 2), OP.subtract)
-        v("scan", r("mx", 0, 16 * NS), r("mk", 0, 16 * NS), r("sa", 0, 16 * NS), 0.0, OP.mult, OP.max)
-        ts(r("fa"), r("mx", 15, 4096, 16), r("thr"), OP.is_lt)
 
-        def totals(k0, k1):
+        def totals(lo, hi, k0, k1):
+            o = r("p3", lo // 2, hi // 2)
             for k in range(k0, k1):
-                pe(r("p3", 0, 128), r("sel", 128 * k, 128 * k + 128), r("sa", 16 + k, 4096, 32), k == 0, False)
-                pe(r("p3", 0, 128), r("nsel", 128 * k, 128 * k + 128), r("sa", k, 4096, 32), False, k == 15)
+                pe(o, r("sel", 128 * k, 128 * k + 128), r("sa", 16 * lo + 16 + k, 16 * hi, 32), k == 0, False)
+                pe(o, r("nsel", 128 * k, 128 * k + 128), r("sa", 16 * lo + k, 16 * hi, 32), False, k == 15)
 
-        def product(k0, k1):
-            for k in range(k0, k1):
-                v("tt", r("sm", 256 * k, 256 * k + 256), r("sa", k, 4096, 16), r("p2", 0, 256), OP.mult)
-                pe(r("p0", 0, 256), r("sel", 128 * k, 128 * k + 128), r("sm", 256 * k, 256 * k + 256), False, k == 15)
-        totals(0, TOT)
-        pe(r("p0", 0, 256), r("dg"), r("one"), True, False)
-        pe(r("p2", 0, 256), r("idm"), r("fa"), True, True)
-        pe(r("p1", 0, 256), r("bb9"), r("fa"), True, True)
-        product(0, 4)
-        ts(r("vi"), r("p1", 0, 256), -40.0, OP.is_lt, 256.0, OP.mult)
+        def block(lo, hi, fp, filler):
+            v("scan", r("mx", 16 * lo, 16 * hi), r("mk", 16 * lo, 16 * hi), r("sa", 16 * lo, 16 * hi), 0.0, OP.mult, OP.max)
+            ts(r("fa", lo, hi), r("mx", 16 * lo + 15, 16 * hi, 16), r("thr"), OP.is_lt)
+            pe(r(fp, lo, hi), r("idm"), r("fa", lo, hi), True, True)
+            pe(r("p1", lo, hi), r("bb9"), r("fa", lo, hi), True, True)
+            pe(r("p0", lo, hi), r("dg"), r("one", lo, hi), True, False)
+            filler()
+            for k in range(16):
+                m = r("sm", 256 * k + lo, 256 * k + hi)
+                v("tt", m, r("sa", 16 * lo + k, 16 * hi, 16), r(fp, lo, hi), OP.mult)
+                pe(r("p0", lo, hi), r("sel", 128 * k, 128 * k + 128), m, False, k == 15)
+                if k == 3:
+                    ts(r("vi", lo, hi), r("p1", lo, hi), -40.0, OP.is_lt, 256.0, OP.mult)
+                    pe(r("p0", lo, hi), r("id"), r("vi", lo, hi), False, False)
+        totals(0, LB, 0, 8)
+        block(0, LB, "p2", lambda: v("tt", r("dj"), r("w", 1, 256, 2), r("w", 0, 256, 2), OP.subtract))
+        totals(0, LB, 8, 13)
+        block(LB, 256, "p7", lambda: ts(r("hi"), r("li"), 6, OP.arith_shift_right))
         act(r("rw", 0, 256), r("p1", 0, 256), AF.Relu, bias=kx(20), scale=-1.0)
-        pe(r("p0", 0, 256), r("id"), r("vi"), False, False)
-        product(4, 16)
-        totals(TOT, 16)
+        totals(0, LB, 13, 16)
+        totals(LB, 256, 0, 16)
         v("tt", r("ab", 0, 256), r("p0", 0, 256), r("hi"), OP.add)
         v("tt", r("ab", 256, 512), r("p0", 0, 256), r("lo"), OP.add)
         v("vt", r("at"), r("ab"))
@@ -376,9 +483,12 @@ def rank_program(g, core, T, topo):
             for a in aa:
                 at[a] = r("p%d" % b, o, o + 16 * (a + 1))
                 o += 16 * (a + 1)
-        for e, b, aa in DED[:4]:
-            for a in aa:
-                pe(at[a], r3("bd", a), r3("fe", slice(0, a + 1)), True, True)
+
+        def equal(banks):
+            for e, b, aa in banks:
+                for a in aa:
+                    pe(at[a], r3("bd", a), r3("fe", slice(0, a + 1)), True, True)
+        equal(DED[:2])
         v("tt", r("p5", 0, 128), r("vi", 0, 256, 2), r("vi", 1, 256, 2), OP.min)
         v("scan", r("ce", 1, 128), r("one", 0, 127), r("p5", 0, 127), 0.0, OP.mult, OP.add)
         v("tt", r("p5", 128, 256), r("p5", 0, 128), r("nc"), OP.mult)
@@ -392,67 +502,100 @@ def rank_program(g, core, T, topo):
         v("tt", r("tg0"), r("tg1"), r("p4", 16, 32), OP.mult)
         v("tt", r("cc", 16, 32), r("ge"), r("cm"), OP.add)
         ts(r("tg"), r("tg0"), -1.0, OP.add)
-        ts(r("jo"), r("p6", 0, 8), 1.0 / 4096, OP.mult)
-        v("copy", ind(r("jw", 256 * t, 256 * t + 256), r("jo")), r("jt"))
-        rid, pid, _ = topo.addr(dst)
-        deps("g", [("jw", 256 * t, 256 * t + 128, 1, False)])
-        g.remote_dma(T.q_jl[:, 128 * t:128 * t + 128], T.q_jw[:, 256 * t:256 * t + 128], T.sem["a%d" % t], T.sem["l%d" % t], pid, rid, topo.mask(core, dst))
-        src = T.cores[(rank - 1 - t % 3) % len(T.cores)]
-        note("a%d" % t, len(topo.engines(src, core)), [("jl", 128 * t, 128 * t + 128, 1, True)])
-        for e, b, aa in DED[4:]:
-            for a in aa:
-                pe(at[a], r3("bd", a), r3("fe", slice(0, a + 1)), True, True)
-        pe(r("p6", 256, 512), r("id8"), r("fa"), True, False)
-        pe(r("p6", 256, 512), r("id"), r("sch"), False, True)
-        for i in range(2):
+        equal(DED[2:4])
+        pe(r("p5", 256, 512), r("id8"), r("fa"), True, False)
+        pe(r("p5", 256, 512), r("id"), r("sch"), False, True)
+        equal(DED[4:])
+
+        def send():
+            ts(r("jo"), r("p6", 0, 8), 1.0 / 4096, OP.mult)
+            v("copy", ind(r("jw", 256 * t, 256 * t + 256), r("jo")), r("jt"))
+            rid, pid, _ = topo.addr(dst)
+            o, i, a, l, m = T.q_jl[:, 128 * t:128 * t + 128], T.q_jw[:, 256 * t:256 * t + 128], "a%d" % t, "l%d" % t, topo.mask(core, dst)
+            ne = len(topo.engines(T.cores[(rank - 1 - t % 3) % len(T.cores)], core))
+            ro, wo = ("jw", 256 * t, 256 * t + 128, 1, False), ("jl", 128 * t, 128 * t + 128, 1, True)
+
+            def issue():
+                deps("g", [ro])
+                g.remote_dma(o, i, T.sem[a], T.sem[l], pid, rid, m)
+                note(a, ne, [wo])
+            ops.append(("g", [ro, wo], 1.0, 3.0, issue))
+
+        def frozen(i):
             v("scan", r("mz", 2048 * i, 2048 * i + 2048), r("mk", 0, 2048), r("sz", 2048 * i, 2048 * i + 2048), 0.0, OP.mult, OP.max)
-        ts(r("fz"), r("mz", 15, 4096, 16), r("thr"), OP.is_lt)
-        pe(r("p1", 256, 512), r("bb9"), r("fz"), True, True)
-        for e, b, aa in DED:
-            for a in aa:
-                if e == "v":
-                    v("red", r("win", a, a + 1), at[a], AxisListType.X, OP.max)
-                else:
-                    act(r("junk", 8 * a * (a + 1), 8 * (a + 1) * (a + 2)), at[a], AF.Relu, bias=r("bias", a, a + 1), accum_out=r("win", a, a + 1))
-        act(r("rw", ZB, ZB + 256), r("p1", 256, 512), AF.Relu, bias=kx(20), scale=-1.0)
-        act(r("nv", 256, 512), r("p6", 256, 512), AF.Relu, bias=kx(21), scale=-1.0)
-        ts(r("nv", 0, 256), r("p6", 256, 512), 63.0, OP.min)
-        jl = r("jl", 128 * t, 128 * t + 128)
-        ts(r("rw", DB0, DB0 + 128), jl, 9.0, OP.add, 1.0, OP.max)
-        ts(r("p5", 0, 128), jl, -0.5, OP.is_gt, -16384.0, OP.mult)
-        v("tt", r("p5", 128, 256), r("w", DB0, DB0 + 128), r("p5", 0, 128), OP.add)
-        v("tt", r("w", DB0, DB0 + 128), r("p5", 128, 256), jl, OP.max)
-        act(r("rg"), ind(r("rw"), POS))
-        if not last:
-            act(r("junk", 2176, 2432), r("vi"), AF.Copy, accum_out=r("vs"))
-        act(r("cb"), ind(r("w"), POS))
-        v("tt", r("wm", 0, 16), r("win"), r("tg"), OP.is_equal)
-        v("tt", r("wm", 16, 32), r("win"), r("tg"), OP.is_equal)
-        v("tt", r("of1"), r("cc"), r("wm"), OP.mult)
-        v("tt", r("of2"), r("of1"), r("tr"), OP.max)
-        v("copy", r("off"), r("of2"))
-        v("copy", ind(r("xt"), r("off")), r("nv"))
+            ts(r("fz", 128 * i, 128 * i + 128), r("mz", 2048 * i + 15, 2048 * i + 2048, 16), r("thr"), OP.is_lt)
+            if i:
+                pe(r("p1", 256, 512), r("bb9"), r("fz"), True, True)
+
+        def frozen_codes():
+            act(r("rw", ZB, ZB + 256), r("p1", 256, 512), AF.Relu, bias=kx(20), scale=-1.0)
+            act(r("rg"), ind(r("rw"), POS))
+            if not last:
+                act(r("junk", 2176, 2432), r("vi"), AF.Copy, accum_out=r("vs"))
+
+        def lowest():
+            for e, b, aa in DED:
+                for a in aa:
+                    if e == "v":
+                        v("red", r("win", a, a + 1), at[a], AxisListType.X, OP.max)
+                    else:
+                        act(r("junk", 8 * a * (a + 1), 8 * (a + 1) * (a + 2)), at[a], AF.Relu, bias=r("bias", a, a + 1), accum_out=r("win", a, a + 1))
+            act(r("nv", 256, 512), r("p5", 256, 512), AF.Relu, bias=kx(21), scale=-1.0)
+            act(r("nv", 0, 256), r("nv", 256, 512), AF.Identity, bias=kx(21), scale=-1.0)
+
+        def arrivals():
+            jl = r("jl", 128 * t, 128 * t + 128)
+            act(r("junk", 2432, 2560), jl, AF.Sign, bias=kx(22), accum_out=r("ns"))
+            ts(r("p5", 0, 128), jl, -0.5, OP.is_gt, -16384.0, OP.mult)
+            v("tt", r("p5", 128, 256), r("w", DB0, DB0 + 128), r("p5", 0, 128), OP.add)
+            v("tt", r("w", DB0, DB0 + 128), r("p5", 128, 256), jl, OP.max)
+            ts(r("nt"), r("dr"), r("ns"), OP.is_ge)
+
+        def moves():
+            v("tt", r("wm", 0, 16), r("win"), r("tg"), OP.is_equal)
+            v("tt", r("wm", 16, 32), r("win"), r("tg"), OP.is_equal)
+            v("tt", r("of1"), r("cc"), r("wm"), OP.mult)
+            v("tt", r("of2"), r("of1"), r("tr"), OP.max)
+            v("copy", r("off"), r("of2"))
+            v("copy", ind(r("xt"), r("off")), r("nv"))
+        frozen(0)
+        frozen(1)
+        send()
+        lowest()
+        frozen_codes()
+        moves()
         if last:
-            dma("y", T.yx[:, 0:2048], r("xt", XW0, XW0 + 2048))
-            dma("y", T.yx[:, 2048:4096], r("xt", XW0 + 2048, XW0 + 4096))
-        else:
+            for i in range(2):
+                dma("y", T.yx[:, 2048 * i:2048 * i + 2048], r("xt", XW0 + 2048 * i, XW0 + 2048 * i + 2048))
+        arrivals()
+
+        def clauses_back():
+            if last:
+                act(r("cb", 0, 512), ind(r("w"), r("pos", 0, 32)))
+                v("copy", r("cb", 512, 1024), ind(r("w"), r("pos", 32, 64)))
+                dma("s", T.yc[:, 0:512], r("cb", 0, 512))
+                dma("y", T.yc[:, 512:1024], r("cb", 512, 1024))
+                return
+            act(r("cb"), ind(r("w"), POS))
             for b in (0, ZB):
-                iota(r("w", b, b + 256), [[0, 256]], 8192, 0)
+                act(r("w", b, b + 256), r("one"), AF.Copy, scale=8192.0)
+        if last:
+            clauses_back()
         pe(r("p6", 0, 64), r("id"), r("fn"), True, False)
         for q in range(16):
             pe(r("p6", 0, 64), r("nsel", 128 * q, 128 * q + 128), r("rg", q, 1024, 16), False, q == 15)
         if not last:
             pe(r("p4", 300, 301), r("onf"), r("vs"), True, True)
-            rank_stage(t + 1, r("p6", 0, 64))
+            rank_stage(t + 1, r("p6", 0, 64), clauses_back)
             v("copy", r("ai", 0, 1), r("p4", 300, 301))
             ts(r("ai", 1, 2), r("ai", 0, 1), 3, OP.bitwise_and)
             v("tt", r("thr"), r("ai", 1, 2), r("thf"), OP.add)
-    dma("s", T.yc[:, :], r("cb"))
-    ts(r("fn"), r("p6", 0, 64), 16.0, OP.add, 0.0, OP.max)
+    new_states(4, r("p6", 0, 64))
     pe(r("p5", 0, 128, P=64), r("fn"), r("id"), True, True)
     ts(r("fo", P=64), r("p5", 0, 128, P=64), 1.0 / 16, OP.mult)
     for gr in range(8):
         dma("y" if gr % 2 == 0 else "s", T.yf[gr:gr + 1, :], r("fo", 16 * gr, 16 * gr + 16, P=64))
+    order()
     for q in "vstg":
         need("g", "e" + q, cnt[q])
     for i in range(nd[0]):

@@ -27,13 +27,14 @@ NDMA = 40
 SEMAPHORES = ["ev", "es", "et", "eg"] + ["a%d" % t for t in range(4)] + ["l%d" % t for t in range(4)] + ["d%d" % i for i in range(NDMA)]
 XW0, XE = 512, 8720
 ZB, DB0, WW = 1024, 2048, 3072
-LS, LB = 96, 128
+LS, LB = 96, 144
 BDS = (2, 3, 4, 5, 6, 7)
 DED = (("s", 0, (15, 14)), ("s", 7, (13, 12)), ("s", 3, (11, 10)), ("s", 2, (9, 8, 7)), ("v", 4, (6, 5, 4, 3, 2, 1, 0)))
 SCOLS = tuple(a for e, b, aa in DED if e == "s" for a in aa)
 
 
-CY, CPE, WAKE, FIX, SLACK, GAMMA, SIGMA = 0.00105, 0.0009, 0.12, 0.01, 0.05, 1.7, 3.5
+CY, CPE, WAKE, FIX, SLACK, GAMMA, SIGMA = 0.00105, 0.0009, 0.11, 0.01, 0.05, 1.7, 3.5
+SEEDS = (313303, 302857, 208832, 398229, 87847, 179512, 39628, 96281, 664645, 136495)
 
 
 def rank_program(g, core, T, topo):
@@ -113,7 +114,7 @@ def rank_program(g, core, T, topo):
                 kk[k] = a
         return acc, real, kk
 
-    ops = []
+    ops, marks = [], []
 
     def cols(a):
         if a[0] == "@":
@@ -176,9 +177,13 @@ def rank_program(g, core, T, topo):
     def order():
         n = len(ops)
         pre = [{} for _ in range(n)]
-        hist = {}
+        hist, gl = {}, []
         for i in range(n):
             q, acc = ops[i][0], ops[i][1]
+            if q == "g":
+                if gl:
+                    pre[i][gl[-1]] = 0.0
+                gl.append(i)
             for (b, lo, hi, st, w) in acc:
                 bank = b[0] == "p" and len(b) == 2
                 hs = hist.setdefault(b, ([], []))
@@ -198,6 +203,12 @@ def rank_program(g, core, T, topo):
         way = [0.0] * n
         for i in range(n - 1, -1, -1):
             way[i] = ops[i][3] + max([way[j] + pre[j][i] for j in post[i]], default=0.0)
+        per = marks[2] - marks[1]
+        for seed in SEEDS:
+            for m in marks:
+                i = m + seed % per if m else marks[1] - per + seed % per
+                if i < n:
+                    way[i] += (seed // per % 64 - 31.5) * 0.15
         left = [len(p) for p in pre]
         ready = {q: {} for q in Q}
         free = {q: 0.0 for q in Q}
@@ -338,11 +349,12 @@ def rank_program(g, core, T, topo):
         v("set", r("onf"), 1.0 / 4096)
         v("set", r("ce", 0, 1), 0.0)
         v("set", r3("ftb", slice(1, 32, 2), 7, 15, 256, 16), 0.0)
-        ts(r("bb9"), r("img"), gc, OP.is_equal, -9.0, OP.mult)
-        ts(r("idm"), r("im"), pc, OP.is_equal, 8192.0, OP.mult)
+        act(r("bb9"), r("bb"), AF.Copy, scale=-9.0)
+        act(r("idm"), r("id"), AF.Copy, scale=8192.0)
 
     def consts_b():
-        ts(r("nsel"), r("sel"), -1.0, OP.mult)
+        for q in range(16):
+            act(r("nsel", 128 * q, 128 * q + 128), r("sel", 128 * q, 128 * q + 128), AF.Copy, scale=-1.0)
         ts(kx(0), qc, -512.0, OP.mult, 7680.0, OP.add)
         ts(kx(2), hb, -1.0, OP.mult, 1.0, OP.add)
         ts(kx(3), qc, 7.0, OP.is_equal)
@@ -350,7 +362,7 @@ def rank_program(g, core, T, topo):
         ts(kx(6), pc, -16.0, OP.add)
         ts(kx(4), kx(3), -256.0, OP.mult, 256.0, OP.add)
         ts(r("dg"), r("im"), pc, OP.is_equal, kx(0), OP.mult)
-        ts(r("id8"), r("im"), pc, OP.is_equal, 8.0, OP.mult)
+        act(r("id8"), r("id"), AF.Copy, scale=8.0)
         for t in range(1, 4):
             for c, st in enumerate(((170 * t) % 1024, (341 * t) % 1024)):
                 ts(kx(8 + (t - 1) * 4 + 2 * c), qc, float(st % 16), OP.is_ge)
@@ -394,6 +406,7 @@ def rank_program(g, core, T, topo):
 
     for t in range(4):
         last = t == 3
+        marks.append(len(ops) if t else 0)
         dst = T.cores[(rank + 1 + t % 3) % len(T.cores)]
         if t:
             v("copy", ind(r("w"), POS), r("cb"))
@@ -449,8 +462,7 @@ def rank_program(g, core, T, topo):
             v("copy", r("di", d, 32, 2), r("scn", 256 * d + 15, 256 * d + 256, 16))
         for f in range(7):
             ts(r3("fti", slice(None), f, f, 256, 8), r("di"), f if f < 6 else 8, OP.arith_shift_right, 1, OP.bitwise_and)
-        ts(r("ddi", 0, 16), r("di", 0, 32, 2), 127, OP.bitwise_and)
-        ts(r("ddi", 16, 32), r("di", 1, 32, 2), 63, OP.bitwise_and)
+        ts(r("ddi", 0, 32), r("di"), 127, OP.bitwise_and)
         ts(r("ddi", 32, 48), r("di", 1, 32, 2), 8, OP.arith_shift_right, 1, OP.bitwise_and)
         ts(r3("ftb", slice(None), slice(0, 7)), r3("fti", slice(None), slice(0, 7)), 2.0, OP.mult, -1.0, OP.add)
         v("copy", r("db"), r("ddi"))
@@ -466,10 +478,10 @@ def rank_program(g, core, T, topo):
             i = (a2 * 2 + g2) * 256 + 128 * m
             return r("qm", i, i + 128)
         for a2 in range(2):
-            pe(r("p4", a2, 16, 2), qmat(a2, 0, 1), r("db", 0, 16, 2), True, False)
-            pe(r("p4", a2, 16, 2), qmat(a2, 1, 1), r("db", 1, 16, 2), False, False)
-            pe(r("p4", a2, 16, 2), qmat(a2, 0, 0), r("db", 16, 32, 2), False, False)
-            pe(r("p4", a2, 16, 2), qmat(a2, 1, 0), r("db", 17, 32, 2), False, True)
+            pe(r("p4", a2, 16, 2), qmat(a2, 0, 1), r("db", 0, 32, 4), True, False)
+            pe(r("p4", a2, 16, 2), qmat(a2, 1, 1), r("db", 2, 32, 4), False, False)
+            pe(r("p4", a2, 16, 2), qmat(a2, 0, 0), r("db", 1, 32, 4), False, False)
+            pe(r("p4", a2, 16, 2), qmat(a2, 1, 0), r("db", 3, 32, 4), False, True)
             pe(r("p4", 16 + a2, 32, 2), qmat(a2, 0, 0), r("db", 32, 48, 2), True, False)
             pe(r("p4", 16 + a2, 32, 2), qmat(a2, 1, 0), r("db", 33, 48, 2), False, True)
         ts(r("p3", 128, 256), r("p3", 0, 128), 0.0, OP.is_gt)

from concourse.mybir import AluOpType as OP, AxisListType, ActivationFunctionType as AF

F4, B2, I4, U2 = "float32", "bfloat16", "int32", "uint16"
SB = {
    "xt": ([128, 8720], B2), "ci": ([128, 1024], I4), "cb": ([128, 1024], F4), "w": ([128, 3072], F4), "rw": ([128, 3072], B2),
    "thi": ([128, 1], I4), "thf": ([128, 1], F4), "thr": ([128, 1], F4), "fr0": ([64, 128], I4), "frb": ([64, 128], B2),
    "fn": ([128, 64], B2), "y": ([128, 64], B2), "fl": ([128, 198], B2), "sc": ([128, 198], F4), "zz": ([128, 198], F4),
    "pf": ([128, 64], F4), "pos": ([128, 64], U2), "fo": ([64, 128], F4),
    "lua": ([128, 256], U2), "luz": ([128, 256], U2), "sa": ([128, 4096], B2), "sz": ([128, 4096], B2), "mx": ([128, 4096], B2), "mz": ([128, 4096], B2),
    "fa": ([128, 256], B2), "fz": ([128, 256], B2), "sm": ([128, 4096], B2), "vi": ([128, 256], B2),
    "li": ([128, 256], I4), "hi": ([128, 256], I4), "lo": ([128, 256], I4), "ab": ([128, 512], F4), "at": ([128, 512], F4), "scn": ([128, 512], F4),
    "di": ([128, 32], I4), "fti": ([128, 32, 8], I4), "ftb": ([128, 32, 8], B2), "fe": ([128, 16, 16], B2), "bd": ([128, 16, 128], B2),
    "ddi": ([128, 48], I4), "db": ([128, 48], B2), "cu": ([128, 16], U2), "cc": ([128, 32], F4), "ge": ([128, 16], F4), "cm": ([128, 16], F4),
    "tg": ([128, 16], F4), "tg0": ([128, 16], F4), "win": ([128, 16], F4), "wm": ([128, 32], F4), "of1": ([128, 32], F4), "of2": ([128, 32], F4), "off": ([128, 32], U2),
    "sch": ([128, 256], B2), "nv": ([128, 512], B2), "junk": ([128, 2560], B2), "dra": ([128, 64], F4), "drb": ([128, 64], F4), "dr": ([128, 64], F4), "nt": ([128, 64], F4), "ns": ([128, 1], F4), "vs": ([128, 1], F4), "ai": ([128, 2], I4),
    "dj": ([128, 128], F4), "jt": ([128, 128], F4), "ce": ([128, 128], B2), "o32": ([128, 128], B2),
    "jo": ([128, 8], U2), "jw": ([128, 1024], F4), "jl": ([128, 512], F4), "rg": ([128, 1024], B2),
    "im": ([128, 128], F4), "img": ([128, 128], F4), "g8": ([128, 8], F4), "ki": ([128, 8], I4), "kf": ([128, 8], F4), "kx": ([128, 32], F4),
    "gi": ([128, 8], B2), "gif": ([128, 8], F4), "mb": ([128, 8], F4), "cbm": ([128, 8], F4), "bb": ([128, 128], B2), "bb9": ([128, 128], B2), "gt": ([128, 128], B2), "lt": ([128, 128], B2),
    "id": ([128, 128], B2), "idm": ([128, 128], B2), "id8": ([128, 128], B2), "dg": ([128, 128], B2), "sel": ([128, 2048], B2), "nsel": ([128, 2048], B2), "qm": ([128, 1024], B2),
    "lw0": ([128, 16], F4), "lw": ([128, 16], F4), "tg1": ([128, 16], F4), "bias": ([128, 16], F4), "tr": ([128, 32], F4), "l70": ([128, 16], F4),
    "nc": ([128, 128], B2), "jc0": ([128, 8], F4), "jc1": ([128, 8], F4), "jc8": ([128, 8], B2), "mk": ([128, 4096], B2), "mk3": ([128, 198], B2), "one": ([128, 256], B2), "onf": ([128, 128], F4),
}
SCRATCH = {"q_" + k: ("sbuf", v[0], v[1]) for k, v in SB.items()}
SCRATCH.update({"q_p%d" % i: ("psum", [128, 512], F4) for i in range(8)})
NDMA = 40
SEMAPHORES = ["ev", "es", "et", "eg"] + ["a%d" % t for t in range(4)] + ["l%d" % t for t in range(4)] + ["d%d" % i for i in range(NDMA)]
XW0, XE = 512, 8720
ZB, DB0, WW = 1024, 2048, 3072
LS, LB = 96, 144
BDS = (2, 3, 4, 5, 6, 7)
DED = (("s", 0, (15, 14)), ("s", 7, (13, 12)), ("s", 3, (11, 10)), ("s", 2, (9, 8, 7)), ("v", 4, (6, 5, 4, 3, 2, 1, 0)))
SCOLS = tuple(a for e, b, aa in DED if e == "s" for a in aa)


CY, CPE, WAKE, FIX, SLACK, GAMMA, SIGMA = 0.00105, 0.0009, 0.11, 0.01, 0.05, 1.7, 3.5
SEEDS = (313303, 302857, 208832, 398229, 87847, 179512, 39628, 96281, 664645, 136495)


def rank_program(g, core, T, topo):
    rank = T.rank_of(core)
    if rank is None:
        return
    Q = {"v": g.vector, "s": g.scalar, "t": g.tensor, "g": g, "y": g.sync}
    cnt = {q: 0 for q in Q}
    know = {q: {} for q in Q}
    snap, log, nd = {}, {}, [0]

    def r(n, lo=None, hi=None, step=1, P=128):
        t = T["q_" + n]
        hi = t.shape[1] if hi is None else hi
        lo = 0 if lo is None else lo
        return (n, t[0:P, lo:hi:step] if step != 1 else t[0:P, lo:hi], lo, hi, step)

    def r3(n, a, b=slice(None), lo=0, hi=1 << 20, st=1):
        t = T["q_" + n]
        return (n, t[:, a, b], lo, hi, st)

    def ind(w, o):
        return ("@", w, o)

    def over(a, b):
        if a[0] >= b[1] or b[0] >= a[1]:
            return False
        return not (a[2] == b[2] and a[2] > 1 and (a[0] - b[0]) % a[2])

    def need(q, src, n):
        k = know[q]
        if k.get(src, 0) >= n:
            return
        Q[q].wait_ge(T.sem[src], n)
        k[src] = n
        for s2, n2 in snap.get((src, n), {}).items():
            if k.get(s2, 0) < n2:
                k[s2] = n2

    def deps(q, acc):
        req = {}
        own = "e" + q
        for (b, lo, hi, st, w) in acc:
            bank = b[0] == "p" and len(b) == 2
            for (src, l2, h2, s2, w2), n in log.get(b, {}).items():
                if src == own:
                    if not (w or w2) or (w and q == "t") or not over((lo, hi, st), (l2, h2, s2)):
                        continue
                elif not bank and (not (w or w2) or not over((lo, hi, st), (l2, h2, s2))):
                    continue
                if req.get(src, 0) < n:
                    req[src] = n
        for src in sorted(req, key=lambda x: (x[0] != "e", x)):
            need(q, src, req[src])

    def note(src, n, acc):
        for (b, lo, hi, st, w) in acc:
            log.setdefault(b, {})[(src, lo, hi, st, w)] = n

    def flat(args, kw):
        acc, real, kk = [], [], {}
        for i, a in enumerate(args):
            if isinstance(a, tuple) and a[0] == "@":
                acc.append((a[1][0],) + a[1][2:] + (i == 0,))
                acc.append((a[2][0],) + a[2][2:] + (False,))
                real.append(a[1][1].indirect(a[2][1]))
            elif isinstance(a, tuple):
                acc.append((a[0],) + a[2:] + (i == 0,))
                real.append(a[1])
            else:
                real.append(a)
        for k, a in kw.items():
            if isinstance(a, tuple):
                acc.append((a[0],) + a[2:] + (k == "accum_out",))
                kk[k] = a[1]
            else:
                kk[k] = a
        return acc, real, kk

    ops, marks = [], []

    def cols(a):
        if a[0] == "@":
            return 16 * cols(a[2])
        return min(-(-(a[3] - a[2]) // a[4]), 256 if a[3] >= 1 << 20 else 1 << 20)

    def cost(q, name, args):
        xs = [a for a in args if isinstance(a, tuple)]
        n = max(cols(a) for a in xs[1:]) if len(xs) > 1 else cols(xs[0])
        names = [a[1][0] if a[0] == "@" else a[0] for a in xs]
        two = all(b in SB and SB[b][1] in (B2, U2) for b in names)
        if name == "mm":
            return max(64, cols(args[2])) * (4 if SB[args[2][0]][1] == F4 else 1) * CPE
        if name == "iota":
            return 0.13 + 2 * cols(args[0]) * CY
        if args[0][0] == "@":
            n *= SIGMA
        elif any(a[0] == "@" for a in xs):
            n *= GAMMA
        elif name == "tt":
            n *= 1 if any(len(b) == 2 and b[0] == "p" for b in names) else 2
        elif name in ("copy", "ts", "scan", "vt", "set") and two:
            n *= 0.5
        return max(n, 64) * CY + FIX

    def do(q, name, *args, **kw):
        acc, real, kk = flat(args, kw)
        e = Q[q]
        f = {"copy": lambda: e.tensor_copy(*real), "tt": lambda: e.tensor_tensor(*real), "ts": lambda: e.tensor_scalar(*real),
             "set": lambda: e.memset(*real), "red": lambda: e.tensor_reduce(*real), "scan": lambda: e.tensor_tensor_scan(*real),
             "vt": lambda: e.transpose(*real), "act": lambda: e.activation(*real, **kk), "mm": lambda: e.matmul(*real),
             "iota": lambda: e.iota(*real, **kk)}[name]

        def issue():
            deps(q, acc)
            cnt[q] += 1
            src = "e" + q
            f().then_inc(T.sem[src], 1)
            snap[(src, cnt[q])] = dict(know[q])
            note(src, cnt[q], acc)
        c = cost(q, name, args)
        ops.append((q, acc, c, c, issue))

    def dma(q, out, in_):
        acc, ap = [], []
        for i, a in enumerate((out, in_)):
            ap.append(a[1] if isinstance(a, tuple) else a)
            if isinstance(a, tuple):
                acc.append((a[0],) + a[2:] + (i == 0,))

        def issue():
            deps(q, acc)
            x = "d%d" % nd[0]
            nd[0] += 1
            Q[q].dma_start(ap[0], ap[1]).then_inc(T.sem[x], 16)
            snap[(x, 16)] = dict(know[q])
            note(x, 16, acc)
        ops.append((q, acc, 0.08, 2.5 + (acc[0][2] - acc[0][1]) / 1000, issue))

    def order():
        n = len(ops)
        pre = [{} for _ in range(n)]
        hist, gl = {}, []
        for i in range(n):
            q, acc = ops[i][0], ops[i][1]
            if q == "g":
                if gl:
                    pre[i][gl[-1]] = 0.0
                gl.append(i)
            for (b, lo, hi, st, w) in acc:
                bank = b[0] == "p" and len(b) == 2
                hs = hist.setdefault(b, ([], []))
                for h in (hs[0], hs[1]) if (w or bank) else (hs[0],):
                    for (j, q2, l2, h2, s2, w2) in h:
                        if bank and q == "t" and q2 == "t":
                            pre[i].setdefault(j, 0.0)
                        elif (bank and q != q2) or ((w or w2) and over((lo, hi, st), (l2, h2, s2))):
                            pre[i][j] = WAKE
            for (b, lo, hi, st, w) in acc:
                hist[b][0 if w else 1].append((i, q, lo, hi, st, w))
        post = [[] for _ in range(n)]
        for i in range(n):
            pre[i].pop(i, None)
            for j in pre[i]:
                post[j].append(i)
        way = [0.0] * n
        for i in range(n - 1, -1, -1):
            way[i] = ops[i][3] + max([way[j] + pre[j][i] for j in post[i]], default=0.0)
        per = marks[2] - marks[1]
        for seed in SEEDS:
            for m in marks:
                i = m + seed % per if m else marks[1] - per + seed % per
                if i < n:
                    way[i] += (seed // per % 64 - 31.5) * 0.15
        left = [len(p) for p in pre]
        ready = {q: {} for q in Q}
        free = {q: 0.0 for q in Q}
        end = [0.0] * n
        for i in range(n):
            if not left[i]:
                ready[ops[i][0]][i] = 0.0
        done = []
        while len(done) < n:
            best = None
            for q in Q:
                if ready[q]:
                    t0 = min(max(free[q], x) for x in ready[q].values())
                    i = max((i for i, x in ready[q].items() if max(free[q], x) <= t0 + SLACK), key=lambda k: way[k])
                    s0 = max(free[q], ready[q][i])
                    if best is None or s0 < best[0]:
                        best = (s0, q, i)
            s0, q, i = best
            del ready[q][i]
            free[q] = s0 + ops[i][2]
            end[i] = s0 + ops[i][3]
            done.append(i)
            for j in post[i]:
                left[j] -= 1
                if not left[j]:
                    ready[ops[j][0]][j] = max(end[k] + w for k, w in pre[j].items())
        for i in done:
            ops[i][4]()

    def v(*a): do("v", *a)
    def pe(*a): do("t", "mm", *a)
    def act(out, in_, f=AF.Copy, **k): do("s", "act", out, in_, f, **k)

    def ts(out, in0, s1, op0, s2=None, op1=None):
        if op1 is None:
            v("ts", out, in0, s1, None, op0)
        else:
            v("ts", out, in0, s1, s2, op0, op1)

    def iota(out, pat, base, ch):
        if out[0] == "ki":
            do("g", "iota", out, pat, base, ch)
        else:
            do("g", "iota", out, pat, base, ch, allow_small_or_imprecise_dtypes=True)

    for gr in range(8):
        dma("y" if gr % 2 == 0 else "s", r("fr0", 16 * gr, 16 * gr + 16, P=64), T.fr[gr:gr + 1, :])
    dma("s", r("ci"), T.cl[:, :])
    for i in range(2):
        dma("y", r("xt", XW0 + 2048 * i, XW0 + 2048 * i + 2048), T.xv[:, 2048 * i:2048 * i + 2048])
    dma("s", r("thi"), T.th[:, :])

    iota(r("ki", 0, 1), [[1, 1]], 0, 1)
    iota(r("im"), [[1, 128]], 0, 0)
    iota(r("img"), [[1, 8], [0, 16]], 0, 0)
    iota(r("g8"), [[1, 8]], 0, 0)
    iota(r("lw0"), [[16, 16]], 0, 0)
    iota(r("w"), [[0, WW]], 8192, 0)
    iota(r("l70"), [[-32, 8], [0, 2]], 0, 0)
    iota(r("jc0"), [[16, 8]], 0, 0)
    iota(r("nc"), [[1, 128]], -255, 0)
    iota(r("rw"), [[0, WW]], 1, 0)
    iota(r("jw"), [[0, 1024]], -20, 0)
    kx = lambda i: r("kx", i, i + 1)
    v("set", r("fl"), 0.0)
    v("set", r("fl", 66, 67), 64.0)
    v("set", r("fl", 132, 133), 128.0)
    v("set", r("mk3"), 1.0)
    v("set", r("mk3", 0, 198, 66), 0.0)
    v("set", kx(7), -32.0)
    v("set", kx(20), -36.0)
    v("set", kx(21), 63.0)
    v("set", kx(22), 0.5)
    v("set", r("mk"), 1.0)
    v("set", r("mk", 0, 4096, 16), 0.0)
    ts(r("ki", 1, 2), r("ki", 0, 1), 15, OP.bitwise_and)
    ts(r("ki", 2, 3), r("ki", 0, 1), 4, OP.arith_shift_right)
    ts(r("ki", 3, 4), r("ki", 0, 1), 31, OP.bitwise_and)
    ts(r("ki", 4, 5), r("ki", 0, 1), 4, OP.arith_shift_right, 1, OP.bitwise_and)
    v("copy", r("kf", 0, 5), r("ki", 0, 5))
    pc, qc, gc, p31, hb = [r("kf", i, i + 1) for i in range(5)]
    ts(r("id"), r("im"), pc, OP.is_equal)
    ts(r("bb"), r("img"), gc, OP.is_equal)
    ts(r("gt"), r("im"), pc, OP.is_gt)
    v("tt", r("lt"), r("gt"), r("bb"), OP.mult)

    def new_states(t, xw):
        if t == 0:
            ts(r("fn"), xw, 0.0, OP.max)
        else:
            ts(r("p6", 64, 128), xw, 16.0, OP.add, 0.0, OP.max)
            v("tt", r("fn"), r("p6", 64, 128), r("nt"), OP.mult)

    def rank_stage(t, xw, then=lambda: None):
        new_states(t, xw)
        act(r("y"), r("fn"), AF.Square, bias=kx(7))
        then()

        def flags(seg, src, thr, st, ki):
            c0 = st // 16
            if st == 0:
                ts(r("fl", seg + 1, seg + 65), r(src), thr, OP.is_lt)
                return
            if c0 < 63:
                ts(r("fl", seg + 2, seg + 65 - c0), r(src, c0 + 1, 64), thr, OP.is_lt)
            ts(r("fl", seg + 65 - c0, seg + 65), r(src, 0, c0), thr, OP.is_lt)
            ts(r("fl", seg + 1, seg + 2), r(src, c0, c0 + 1), thr, OP.is_lt, kx(ki), OP.mult)
            ts(r("fl", seg + 65, seg + 66), r(src, c0, c0 + 1), thr, OP.is_lt, kx(ki + 1), OP.mult)
        a0, z0 = (170 * t) % 1024, (341 * t) % 1024
        flags(0, "fn", 8.0, a0, 8 + (t - 1) * 4)
        ts(r("fl", 133, 197), r("fn"), 56.0, OP.is_gt)
        flags(66, "y", 512.0, z0, 10 + (t - 1) * 4)
        pe(r("p5", 256, 454), r("bb"), r("fl"), True, True)
        pe(r("p5", 0, 198), r("lt"), r("fl"), True, True)
        v("scan", r("sc"), r("mk3"), r("p5", 256, 454), 0.0, OP.mult, OP.add)
        v("tt", r("p6", 256, 453), r("sc", 0, 197), r("p5", 1, 198), OP.add)
        v("tt", r("zz", 0, 197), r("p6", 256, 453), r("fl", 1, 198), OP.mult)

        def add(lo, hi, src, at):
            if hi > lo:
                v("tt", r("pf", lo, hi), r(src[0], src[1] + lo, src[1] + hi), r("zz", at, at + hi - lo), OP.add)

        def merge(seg, st, src):
            c0 = st // 16
            if st == 0:
                add(0, 64, src, seg)
                return
            add(c0 + 1, 64, src, seg + 1)
            add(0, c0, src, seg + 64 - c0)
            add(c0, c0 + 1, src, seg)
            add(c0, c0 + 1, ("pf", 0), seg + 64)
        merge(0, a0, ("zz", 132))
        merge(66, z0, ("pf", 0))
        v("copy", r("pos"), r("pf"))

    def consts_a():
        v("set", r("one"), 1.0)
        v("set", r("onf"), 1.0 / 4096)
        v("set", r("ce", 0, 1), 0.0)
        v("set", r3("ftb", slice(1, 32, 2), 7, 15, 256, 16), 0.0)
        act(r("bb9"), r("bb"), AF.Copy, scale=-9.0)
        act(r("idm"), r("id"), AF.Copy, scale=8192.0)

    def consts_b():
        for q in range(16):
            act(r("nsel", 128 * q, 128 * q + 128), r("sel", 128 * q, 128 * q + 128), AF.Copy, scale=-1.0)
        ts(kx(0), qc, -512.0, OP.mult, 7680.0, OP.add)
        ts(kx(2), hb, -1.0, OP.mult, 1.0, OP.add)
        ts(kx(3), qc, 7.0, OP.is_equal)
        ts(kx(5), pc, 16.0, OP.add)
        ts(kx(6), pc, -16.0, OP.add)
        ts(kx(4), kx(3), -256.0, OP.mult, 256.0, OP.add)
        ts(r("dg"), r("im"), pc, OP.is_equal, kx(0), OP.mult)
        act(r("id8"), r("id"), AF.Copy, scale=8.0)
        for t in range(1, 4):
            for c, st in enumerate(((170 * t) % 1024, (341 * t) % 1024)):
                ts(kx(8 + (t - 1) * 4 + 2 * c), qc, float(st % 16), OP.is_ge)
                ts(kx(9 + (t - 1) * 4 + 2 * c), qc, float(st % 16), OP.is_lt)
        ts(r("gif"), r("g8"), gc, OP.is_equal)
        ts(r("mb"), r("gif"), kx(4), OP.mult)
        ts(r("cbm"), r("gif"), kx(3), OP.mult)
        for a2 in range(2):
            for g2 in range(2):
                x = (pc, kx(5), kx(6))[(g2 - a2) % 3]
                i = (a2 * 2 + g2) * 256
                ts(r("qm", i, i + 128), r("im"), x, OP.is_equal, (kx(2), hb)[a2], OP.mult)
                ts(r("qm", i + 128, i + 256), r("qm", i, i + 128), 64.0, OP.mult)
        ts(r("lw"), r("lw0"), qc, OP.add)
        ts(r("tg1"), r("lw"), -1.0, OP.mult, 3585.0, OP.add)
        for a in SCOLS:
            v("set", r("tg1", a, a + 1), 1.0)
        ts(r("bias"), r("lw"), -3584.0, OP.add)
        v("copy", r("tr", 0, 16), r("lw"))
        ts(r("tr", 16, 32), r("lw"), 256.0, OP.add)
        ts(r3("ftb", slice(0, 32, 2), 7, 7, 256, 16), r("l70"), p31, OP.subtract)
        ts(r("jc1"), r("jc0"), qc, OP.add)
        ts(r("jc8"), r("jc1"), -4096.0, OP.mult, 4096.0 * 255, OP.add)
        v("copy", r("thf"), r("thi"))
        v("copy", r("thr"), r("thi"))

    ts(r("gi"), r("g8"), gc, OP.is_equal)
    v("set", r("sel"), 0.0)
    for q in range(16):
        act(r("sel", q * 129, q * 128 + 128, 16), r("gi"))
    ts(r("frb", P=64), r("fr0", P=64), 16.0, OP.mult)
    pe(r("p6", 0, 64), r("frb", P=64), ("id", T.q_id[0:64, 0:64], 0, 64, 1), True, True)
    v("set", r("xt", 8704, 8720), 63.0)
    rank_stage(0, r("p6", 0, 64))
    POS = r("pos")
    XG = r("xt", XW0, XE)
    for i in range(2):
        act(r("xt", 4608 + 2048 * i, 6656 + 2048 * i), r("xt", 512 + 2048 * i, 2560 + 2048 * i), AF.Identity, scale=-1.0, bias=kx(21))
    consts_a()
    v("copy", ind(r("w"), POS), r("ci"))

    for t in range(4):
        last = t == 3
        marks.append(len(ops) if t else 0)
        dst = T.cores[(rank + 1 + t % 3) % len(T.cores)]
        if t:
            v("copy", ind(r("w"), POS), r("cb"))
        for lo, hi in ((0, LS), (LS, 256)):
            v("copy", r("lua", lo, hi), r("w", lo, hi))
            if lo:
                lo = LB
            act(r("sa", 16 * lo, 16 * hi), ind(XG, r("lua", lo, hi)))
        v("copy", r("sa", 16 * LS, 16 * LB), ind(XG, r("lua", LS, LB)))
        v("copy", r("luz"), r("w", ZB, ZB + 256))
        for i in range(2):
            act(r("sz", 2048 * i, 2048 * i + 2048), ind(XG, r("luz", 128 * i, 128 * i + 128)))
        ts(r("dra"), r("zz", 132, 196), 1.0, OP.is_lt, 1e5, OP.mult)
        ts(r("drb"), r("zz", 132, 196), 2.0, OP.mult, -4224.0, OP.add)
        v("tt", r("dr"), r("dra"), r("drb"), OP.add)
        if t == 0:
            consts_b()
        v("copy", r("li"), r("w", 0, 256))
        ts(r("lo"), r("li"), 63, OP.bitwise_and)

        def totals(lo, hi, k0, k1):
            o = r("p3", lo // 2, hi // 2)
            for k in range(k0, k1):
                pe(o, r("sel", 128 * k, 128 * k + 128), r("sa", 16 * lo + 16 + k, 16 * hi, 32), k == 0, False)
                pe(o, r("nsel", 128 * k, 128 * k + 128), r("sa", 16 * lo + k, 16 * hi, 32), False, k == 15)

        def block(lo, hi, fp, filler):
            v("scan", r("mx", 16 * lo, 16 * hi), r("mk", 16 * lo, 16 * hi), r("sa", 16 * lo, 16 * hi), 0.0, OP.mult, OP.max)
            ts(r("fa", lo, hi), r("mx", 16 * lo + 15, 16 * hi, 16), r("thr"), OP.is_lt)
            pe(r(fp, lo, hi), r("idm"), r("fa", lo, hi), True, True)
            pe(r("p1", lo, hi), r("bb9"), r("fa", lo, hi), True, True)
            pe(r("p0", lo, hi), r("dg"), r("one", lo, hi), True, False)
            filler()
            for k in range(16):
                m = r("sm", 256 * k + lo, 256 * k + hi)
                v("tt", m, r("sa", 16 * lo + k, 16 * hi, 16), r(fp, lo, hi), OP.mult)
                pe(r("p0", lo, hi), r("sel", 128 * k, 128 * k + 128), m, False, k == 15)
                if k == 3:
                    ts(r("vi", lo, hi), r("p1", lo, hi), -40.0, OP.is_lt, 256.0, OP.mult)
                    pe(r("p0", lo, hi), r("id"), r("vi", lo, hi), False, False)
        totals(0, LB, 0, 8)
        block(0, LB, "p2", lambda: v("tt", r("dj"), r("w", 1, 256, 2), r("w", 0, 256, 2), OP.subtract))
        totals(0, LB, 8, 13)
        block(LB, 256, "p7", lambda: ts(r("hi"), r("li"), 6, OP.arith_shift_right))
        act(r("rw", 0, 256), r("p1", 0, 256), AF.Relu, bias=kx(20), scale=-1.0)
        totals(0, LB, 13, 16)
        totals(LB, 256, 0, 16)
        v("tt", r("ab", 0, 256), r("p0", 0, 256), r("hi"), OP.add)
        v("tt", r("ab", 256, 512), r("p0", 0, 256), r("lo"), OP.add)
        v("vt", r("at"), r("ab"))
        v("scan", r("scn"), r("mk", 0, 512), r("at"), 0.0, OP.mult, OP.max)
        for d in range(2):
            v("copy", r("di", d, 32, 2), r("scn", 256 * d + 15, 256 * d + 256, 16))
        for f in range(7):
            ts(r3("fti", slice(None), f, f, 256, 8), r("di"), f if f < 6 else 8, OP.arith_shift_right, 1, OP.bitwise_and)
        ts(r("ddi", 0, 32), r("di"), 127, OP.bitwise_and)
        ts(r("ddi", 32, 48), r("di", 1, 32, 2), 8, OP.arith_shift_right, 1, OP.bitwise_and)
        ts(r3("ftb", slice(None), slice(0, 7)), r3("fti", slice(None), slice(0, 7)), 2.0, OP.mult, -1.0, OP.add)
        v("copy", r("db"), r("ddi"))
        v("vt", r3("fe", slice(None)), r3("ftb", slice(None)))
        for gr in range(8):
            o = r3("bd", slice(None), slice(16 * gr, 16 * gr + 16), 16 * gr, 16 * gr + 16)
            if gr in BDS:
                act(o, r3("fe", slice(None)), AF.Identity, bias=r("cbm", gr, gr + 1), scale=r("mb", gr, gr + 1))
            else:
                ts(o, r3("fe", slice(None)), r("mb", gr, gr + 1), OP.mult, r("cbm", gr, gr + 1), OP.add)

        def qmat(a2, g2, m):
            i = (a2 * 2 + g2) * 256 + 128 * m
            return r("qm", i, i + 128)
        for a2 in range(2):
            pe(r("p4", a2, 16, 2), qmat(a2, 0, 1), r("db", 0, 32, 4), True, False)
            pe(r("p4", a2, 16, 2), qmat(a2, 1, 1), r("db", 2, 32, 4), False, False)
            pe(r("p4", a2, 16, 2), qmat(a2, 0, 0), r("db", 1, 32, 4), False, False)
            pe(r("p4", a2, 16, 2), qmat(a2, 1, 0), r("db", 3, 32, 4), False, True)
            pe(r("p4", 16 + a2, 32, 2), qmat(a2, 0, 0), r("db", 32, 48, 2), True, False)
            pe(r("p4", 16 + a2, 32, 2), qmat(a2, 1, 0), r("db", 33, 48, 2), False, True)
        ts(r("p3", 128, 256), r("p3", 0, 128), 0.0, OP.is_gt)
        v("tt", r("p3", 256, 384), r("dj"), r("p3", 128, 256), OP.mult)
        v("tt", r("jt"), r("p3", 256, 384), r("w", 0, 256, 2), OP.add)
        v("copy", r("cu"), r("p4", 0, 16))
        act(r("sch"), ind(XG, r("cu")))
        at = {}
        for e, b, aa in DED:
            o = 32 if b == 4 else 0
            for a in aa:
                at[a] = r("p%d" % b, o, o + 16 * (a + 1))
                o += 16 * (a + 1)

        def equal(banks):
            for e, b, aa in banks:
                for a in aa:
                    pe(at[a], r3("bd", a), r3("fe", slice(0, a + 1)), True, True)
        equal(DED[:2])
        v("tt", r("p5", 0, 128), r("vi", 0, 256, 2), r("vi", 1, 256, 2), OP.min)
        v("scan", r("ce", 1, 128), r("one", 0, 127), r("p5", 0, 127), 0.0, OP.mult, OP.add)
        v("tt", r("p5", 128, 256), r("p5", 0, 128), r("nc"), OP.mult)
        v("tt", r("o32"), r("p5", 128, 256), r("ce"), OP.add)
        pe(r("p6", 0, 8), r("id"), r("jc8"), True, False)
        for q in range(16):
            pe(r("p6", 0, 8), r("sel", 128 * q, 128 * q + 128), r("o32", q, 128, 16), False, q == 15)
        ts(r("cc", 0, 16), r("p4", 0, 16), 512.0, OP.add)
        ts(r("ge"), r("p4", 0, 16), 4096.0, OP.is_lt, 8192.0, OP.mult)
        ts(r("cm"), r("p4", 0, 16), -3584.0, OP.add)
        v("tt", r("tg0"), r("tg1"), r("p4", 16, 32), OP.mult)
        v("tt", r("cc", 16, 32), r("ge"), r("cm"), OP.add)
        ts(r("tg"), r("tg0"), -1.0, OP.add)
        equal(DED[2:4])
        pe(r("p5", 256, 512), r("id8"), r("fa"), True, False)
        pe(r("p5", 256, 512), r("id"), r("sch"), False, True)
        equal(DED[4:])

        def send():
            ts(r("jo"), r("p6", 0, 8), 1.0 / 4096, OP.mult)
            v("copy", ind(r("jw", 256 * t, 256 * t + 256), r("jo")), r("jt"))
            rid, pid, _ = topo.addr(dst)
            o, i, a, l, m = T.q_jl[:, 128 * t:128 * t + 128], T.q_jw[:, 256 * t:256 * t + 128], "a%d" % t, "l%d" % t, topo.mask(core, dst)
            ne = len(topo.engines(T.cores[(rank - 1 - t % 3) % len(T.cores)], core))
            ro, wo = ("jw", 256 * t, 256 * t + 128, 1, False), ("jl", 128 * t, 128 * t + 128, 1, True)

            def issue():
                deps("g", [ro])
                g.remote_dma(o, i, T.sem[a], T.sem[l], pid, rid, m)
                note(a, ne, [wo])
            ops.append(("g", [ro, wo], 1.0, 3.0, issue))

        def frozen(i):
            v("scan", r("mz", 2048 * i, 2048 * i + 2048), r("mk", 0, 2048), r("sz", 2048 * i, 2048 * i + 2048), 0.0, OP.mult, OP.max)
            ts(r("fz", 128 * i, 128 * i + 128), r("mz", 2048 * i + 15, 2048 * i + 2048, 16), r("thr"), OP.is_lt)
            if i:
                pe(r("p1", 256, 512), r("bb9"), r("fz"), True, True)

        def frozen_codes():
            act(r("rw", ZB, ZB + 256), r("p1", 256, 512), AF.Relu, bias=kx(20), scale=-1.0)
            act(r("rg"), ind(r("rw"), POS))
            if not last:
                act(r("junk", 2176, 2432), r("vi"), AF.Copy, accum_out=r("vs"))

        def lowest():
            for e, b, aa in DED:
                for a in aa:
                    if e == "v":
                        v("red", r("win", a, a + 1), at[a], AxisListType.X, OP.max)
                    else:
                        act(r("junk", 8 * a * (a + 1), 8 * (a + 1) * (a + 2)), at[a], AF.Relu, bias=r("bias", a, a + 1), accum_out=r("win", a, a + 1))
            act(r("nv", 256, 512), r("p5", 256, 512), AF.Relu, bias=kx(21), scale=-1.0)
            act(r("nv", 0, 256), r("nv", 256, 512), AF.Identity, bias=kx(21), scale=-1.0)

        def arrivals():
            jl = r("jl", 128 * t, 128 * t + 128)
            act(r("junk", 2432, 2560), jl, AF.Sign, bias=kx(22), accum_out=r("ns"))
            ts(r("p5", 0, 128), jl, -0.5, OP.is_gt, -16384.0, OP.mult)
            v("tt", r("p5", 128, 256), r("w", DB0, DB0 + 128), r("p5", 0, 128), OP.add)
            v("tt", r("w", DB0, DB0 + 128), r("p5", 128, 256), jl, OP.max)
            ts(r("nt"), r("dr"), r("ns"), OP.is_ge)

        def moves():
            v("tt", r("wm", 0, 16), r("win"), r("tg"), OP.is_equal)
            v("tt", r("wm", 16, 32), r("win"), r("tg"), OP.is_equal)
            v("tt", r("of1"), r("cc"), r("wm"), OP.mult)
            v("tt", r("of2"), r("of1"), r("tr"), OP.max)
            v("copy", r("off"), r("of2"))
            v("copy", ind(r("xt"), r("off")), r("nv"))
        frozen(0)
        frozen(1)
        send()
        lowest()
        frozen_codes()
        moves()
        if last:
            for i in range(2):
                dma("y", T.yx[:, 2048 * i:2048 * i + 2048], r("xt", XW0 + 2048 * i, XW0 + 2048 * i + 2048))
        arrivals()

        def clauses_back():
            if last:
                act(r("cb", 0, 512), ind(r("w"), r("pos", 0, 32)))
                v("copy", r("cb", 512, 1024), ind(r("w"), r("pos", 32, 64)))
                dma("s", T.yc[:, 0:512], r("cb", 0, 512))
                dma("y", T.yc[:, 512:1024], r("cb", 512, 1024))
                return
            act(r("cb"), ind(r("w"), POS))
            for b in (0, ZB):
                act(r("w", b, b + 256), r("one"), AF.Copy, scale=8192.0)
        if last:
            clauses_back()
        pe(r("p6", 0, 64), r("id"), r("fn"), True, False)
        for q in range(16):
            pe(r("p6", 0, 64), r("nsel", 128 * q, 128 * q + 128), r("rg", q, 1024, 16), False, q == 15)
        if not last:
            pe(r("p4", 300, 301), r("onf"), r("vs"), True, True)
            rank_stage(t + 1, r("p6", 0, 64), clauses_back)
            v("copy", r("ai", 0, 1), r("p4", 300, 301))
            ts(r("ai", 1, 2), r("ai", 0, 1), 3, OP.bitwise_and)
            v("tt", r("thr"), r("ai", 1, 2), r("thf"), OP.add)
    new_states(4, r("p6", 0, 64))
    pe(r("p5", 0, 128, P=64), r("fn"), r("id"), True, True)
    ts(r("fo", P=64), r("p5", 0, 128, P=64), 1.0 / 16, OP.mult)
    for gr in range(8):
        dma("y" if gr % 2 == 0 else "s", T.yf[gr:gr + 1, :], r("fo", 16 * gr, 16 * gr + 16, P=64))
    order()
    for q in "vstg":
        need("g", "e" + q, cnt[q])
    for i in range(nd[0]):
        need("g", "d%d" % i, 16)
    for t in range(4):
        d = T.cores[(rank + 1 + t % 3) % len(T.cores)]
        need("g", "l%d" % t, len(topo.engines(core, d)))
